import numpy as np
import ml_dtypes


def mxq(x, axis, fmt="e4m3"):
    dtype, down = {"e4m3": (ml_dtypes.float8_e4m3fn, 7), "e5m2": (ml_dtypes.float8_e5m2, 14)}[fmt]
    v = np.moveaxis(np.asarray(x, np.float32).astype(ml_dtypes.bfloat16).astype(np.float64), axis, -1)
    blocks = v.reshape(v.shape[:-1] + (-1, 32))
    amax = np.abs(blocks).max(-1, keepdims=True)
    byte = np.maximum(np.where(amax > 0, np.frexp(amax)[1] - 1 + 127, 0) - down, 1)
    scale = np.exp2(byte - 127.0)
    codes = (blocks / scale).astype(np.float32).astype(dtype).astype(np.float64)
    return np.moveaxis((codes * scale).reshape(v.shape), -1, axis)


WIDE = False


def mx_kscale(k):
    if not WIDE:
        return np.ones(k)
    levels = np.array([10, -10, 5, -5, 0])
    if k % 512:
        return np.exp2(np.random.permutation(np.resize(levels, k // 32))).repeat(32)
    a = np.empty((k // 512, 16))
    for p in range(k // 512):
        a[p, :8] = np.random.permutation(np.resize(levels, 8))
        for g in range(8):
            far = levels[np.abs(levels - a[p, g]) >= 10]
            a[p, g + 8] = far[np.random.randint(len(far))]
    return np.exp2(a.ravel()).repeat(32)


def f64(x):
    return np.asarray(x).astype(np.float64)


def striped(idx):
    return np.tile(idx.reshape(-1, 16).T, (8, 1)).astype(np.uint16)


def unstriped(offs):
    return offs[:16].T.reshape(-1).astype(np.int64)


E2M1 = np.array([0.0, 0.5, 1.0, 1.5, 2.0, 3.0, 4.0, 6.0, -0.0, -0.5, -1.0, -1.5, -2.0, -3.0, -4.0, -6.0])


def pack_fp4(w):
    k, n = w.shape
    w = f64(np.asarray(w, np.float32).astype(ml_dtypes.bfloat16)).reshape(k // 32, 32, n)
    amax = np.abs(w).max(1)
    mant, ex = np.frexp(amax / 6.0)
    byte = np.clip(np.where(amax > 0, np.where(mant > 0.5, ex, ex - 1) + 127, 1), 1, 254)
    scaled = (w * np.exp2(127.0 - byte)[:, None, :]).reshape(k, n).astype(np.float32)
    c = np.ascontiguousarray(scaled.reshape(k // 512, 128, 4, n).transpose(0, 1, 3, 2)).astype(ml_dtypes.float4_e2m1fn).view(np.uint8) & 0xF
    words = (c[..., 0::2] | (c[..., 1::2] << 4)).reshape(k // 512, 128, 2 * n)
    return np.ascontiguousarray(words), np.ascontiguousarray(byte.astype(np.uint8).reshape(k // 512, 16, n))


def unpack_fp4(words, scales):
    g, _, n = scales.shape
    words = np.ascontiguousarray(words).reshape(g, 128, n, 2)
    nib = np.empty((g, 128, n, 4), np.uint8)
    nib[..., 0::2] = words & 0xF
    nib[..., 1::2] = words >> 4
    vals = E2M1[nib] * np.repeat(np.exp2(scales.astype(np.float64) - 127.0), 8, axis=1)[..., None]
    return vals.transpose(0, 1, 3, 2).reshape(g * 512, n)


def planes(y):
    n, m = y.shape
    v = y.astype(np.float32).astype(ml_dtypes.bfloat16).astype(np.float64).reshape(n // 32, 32, m)
    top = np.abs(v).max(1)
    byte = np.clip(np.where(top > 0, np.frexp(top)[1] - 1 + 127 - 7, 1), 1, 254)
    codes = (v * np.exp2(127.0 - byte)[:, None, :]).reshape(n, m).astype(np.float32).astype(ml_dtypes.float8_e4m3fn).view(np.uint8)
    words = codes.reshape(n // 512, 128, 4, m).transpose(0, 1, 3, 2)
    return np.ascontiguousarray(words), np.ascontiguousarray(byte.astype(np.uint8).reshape(n // 512, 16, m))


K, T, N, U = 1024, 1024, 512, 2048


def setup_inputs():
    n = np.random.standard_normal
    s = mx_kscale(K)[:, None]
    packed_xT = pack_fp4(n((K, T)) * s)
    return {
        "x_words": packed_xT[0],
        "x_scales": packed_xT[1],
        "mem": n((N, U)).astype(np.float32),
        "w1": (n((K, N)) / np.sqrt(K) / s).astype(np.float32),
        "slot": striped(np.random.permutation(U)[:T]),
    }


def reference(x_words, x_scales, mem, w1, slot):
    xq = unpack_fp4(x_words, x_scales)
    y = mxq(f64(w1), 0, "e4m3").T @ xq
    out = f64(mem).copy()
    out[:, unstriped(slot)] = y
    return (out,) + planes(out)

@@ -1,0 +1,137 @@
+from contextlib import ExitStack
+
+import concourse.mybir as mybir
+
+K, T, N, U = 1024, 1024, 512, 2048
+FLOPS = 2 * K * T * N
+
+F32 = mybir.dt.float32
+BF16 = mybir.dt.bfloat16
+I32 = mybir.dt.int32
+U32 = mybir.dt.uint32
+U16 = mybir.dt.uint16
+U8 = mybir.dt.uint8
+FP8X4 = mybir.dt.float8_e4m3fn_x4
+FP4X4 = mybir.dt.float4_e2m1fn_x4
+
+P = 128
+PACK = 4
+PASSES = K // (P * PACK)
+BANK = 512
+HALVES = T // BANK
+VECTOR_COLS = 1152
+VECTOR_PIECES = ((0, 512), (512, 1024), (1024, 1152))
+SCALAR_PIECES = ((1152, 1536), (1536, 2048))
+QUANT_PIECES = ((0, 512), (512, 1024), (1024, 1536), (1536, 2048))
+
+
+def tile_picked_wkvput_none_lo_kernel(tc, x_words, x_scales, mem, w1, slot, out_0, out_1, out_2):
+    nc = tc.nc
+    with ExitStack() as ctx:
+        keep = ctx.enter_context(tc.tile_pool(name="keep", bufs=1))
+        psum = ctx.enter_context(tc.psum_pool(name="psum", bufs=1))
+
+        offsets = keep.tile([P, T // 16], U16, name="offsets")
+        w_raw = [keep.tile([P, PACK, N], F32, name="w_raw%d" % g) for g in range(PASSES)]
+        w_bf = [keep.tile([P, PACK * N], BF16, name="w_bf%d" % g, align_bytes=64) for g in range(PASSES)]
+        w_codes = [keep.tile([P, N], U32, name="w_codes%d" % g, tag="codes%d" % g, align_bytes=64) for g in range(PASSES)]
+        w_scales = [keep.tile([P, N], U8, name="w_scales%d" % g, align_bytes=64) for g in range(PASSES)]
+        x_codes = [keep.tile([P, PASSES, 2 * BANK], U8, name="x_codes%d" % h, align_bytes=64) for h in range(HALVES)]
+        x_sc = [keep.tile([P, PASSES, BANK], U8, name="x_sc%d" % h, align_bytes=64) for h in range(HALVES)]
+        window = [keep.tile([P, U], F32, name="window%d" % t) for t in range(PACK)]
+        y = [keep.tile([P, T], F32, name="y%d" % t) for t in range(PACK)]
+        out_codes = keep.tile([P, U], U32, name="out_codes", align_bytes=64)
+        out_scales = keep.tile([P, U], U8, name="out_scales", align_bytes=64)
+
+        mem_rows = mem.rearrange("(p t) c -> p t c", t=PACK)
+        out_rows = out_0.rearrange("(p t) c -> p t c", t=PACK)
+
+        def load_w(g):
+            nc.sync.dma_start(out=w_raw[g][:], in_=w1[512 * g : 512 * (g + 1), :].rearrange("(p j) n -> p j n", j=PACK))
+
+        def load_x(h):
+            for q in range(4):
+                rows = x_scales[:, 4 * q : 4 * q + 4, BANK * h : BANK * (h + 1)].rearrange("g r n -> r g n")
+                nc.sync.dma_start(out=x_sc[h][32 * q : 32 * q + 4, :, :].bitcast(I32), in_=rows.bitcast(I32))
+            src = x_words[:, :, 2 * BANK * h : 2 * BANK * (h + 1)].rearrange("g p n -> p g n")
+            nc.sync.dma_start(out=x_codes[h][:].bitcast(I32), in_=src.bitcast(I32))
+
+        load_w(0)
+        load_w(1)
+        load_x(0)
+        nc.sync.dma_start(offsets[:], slot)
+        nc.sync.dma_start(out=window[0][:], in_=mem_rows[:, 0, :])
+        load_x(1)
+        for t in range(1, PACK):
+            nc.sync.dma_start(out=window[t][:], in_=mem_rows[:, t, :])
+
+        def deal_w(copy, g, t0, t1):
+            dst = w_bf[g][:].rearrange("p (t m j) -> p m j t", t=PACK, j=PACK)
+            src = w_raw[g][:].rearrange("p j (m t) -> p m j t", t=PACK)
+            copy(out=dst[:, :, :, t0:t1], in_=src[:, :, :, t0:t1])
+
+        def quantize_w(g, t0, t1):
+            nc.vector.quantize_mx(
+                out=w_codes[g][:, P * t0 : P * t1].bitcast(FP8X4),
+                scales=w_scales[g][:, P * t0 : P * t1],
+                in_=w_bf[g][:, PACK * P * t0 : PACK * P * t1],
+            )
+
+        for g in range(PASSES):
+            deal_w(nc.vector.tensor_copy, g, 0, 2)
+            deal_w(nc.scalar.copy, g, 2, 4)
+            quantize_w(g, 0, 2)
+            quantize_w(g, 2, 4)
+
+        for t in range(PACK):
+            for h in range(HALVES):
+                acc = psum.tile([P, BANK], F32, name="acc%d_%d" % (t, h))
+                for g in range(PASSES):
+                    nc.tensor.matmul_mx(
+                        out=acc[:],
+                        lhsT=w_codes[g][:, P * t : P * (t + 1)].bitcast(FP8X4),
+                        lhsT_scale=w_scales[g][:, P * t : P * (t + 1)],
+                        rhs=x_codes[h][:, g, :].bitcast(FP4X4),
+                        rhs_scale=x_sc[h][:, g, :],
+                        start=(g == 0),
+                        stop=(g == PASSES - 1),
+                    )
+                nc.scalar.copy(out=y[t][:, BANK * h : BANK * (h + 1)], in_=acc[:])
+
+        grouped = keep.tile([P, U * PACK], BF16, name="grouped", tag="codes1", align_bytes=64)
+        by_col = grouped[:].rearrange("p (c t) -> p c t", t=PACK)
+
+        for t in range(PACK):
+            if t == 0:
+                for h in range(HALVES):
+                    cols = BANK // 16
+                    nc.vector.tensor_copy(
+                        window[t][:].indirect(offsets[:, cols * h : cols * (h + 1)]), y[t][:, BANK * h : BANK * (h + 1)]
+                    )
+            else:
+                nc.vector.tensor_copy(window[t][:].indirect(offsets[:]), y[t][:])
+            nc.sync.dma_start(out=out_rows[:, t, :], in_=window[t][:])
+            if t < 2:
+                nc.scalar.copy(out=by_col[:, :, t], in_=window[t][:])
+            elif t == 2:
+                twice = window[t][:, 0:VECTOR_COLS].unsqueeze(2).to_broadcast([P, VECTOR_COLS, 2])
+                nc.scalar.copy(out=by_col[:, 0:VECTOR_COLS, 2:4], in_=twice)
+                nc.scalar.copy(out=by_col[:, VECTOR_COLS:U, 2], in_=window[t][:, VECTOR_COLS:U])
+
+        last = PACK - 1
+        for c0, c1 in VECTOR_PIECES:
+            nc.vector.tensor_copy(out=by_col[:, c0:c1, last], in_=window[last][:, c0:c1])
+        for c0, c1 in SCALAR_PIECES:
+            nc.scalar.copy(out=by_col[:, c0:c1, last], in_=window[last][:, c0:c1])
+        words_out = out_1[0].rearrange("p c r -> p (c r)").bitcast(I32)
+        for c0, c1 in QUANT_PIECES:
+            nc.vector.quantize_mx(
+                out=out_codes[:, c0:c1].bitcast(FP8X4),
+                scales=out_scales[:, c0:c1],
+                in_=grouped[:, PACK * c0 : PACK * c1],
+            )
+            nc.sync.dma_start(out=words_out[:, c0:c1], in_=out_codes[:, c0:c1].bitcast(I32))
+        for q in range(4):
+            nc.scalar.dma_start(
+                out=out_2[0, 4 * q : 4 * q + 4, :].bitcast(I32), in_=out_scales[32 * q : 32 * q + 4, :].bitcast(I32)
+            )

@@ -19,10 +19,10 @@ PACK = 4
 PASSES = K // (P * PACK)
 BANK = 512
 HALVES = T // BANK
-VECTOR_COLS = 1152
-VECTOR_PIECES = ((0, 512), (512, 1024), (1024, 1152))
-SCALAR_PIECES = ((1152, 1536), (1536, 2048))
-QUANT_PIECES = ((0, 512), (512, 1024), (1024, 1536), (1536, 2048))
+VECTOR_COLS = 1024
+VECTOR_PIECES = ((0, 512), (512, 1024))
+SCALAR_PIECES = ((1024, 1536), (1536, 1792), (1792, 2048))
+QUANT_PIECES = VECTOR_PIECES + SCALAR_PIECES
 
 
 def tile_picked_wkvput_none_lo_kernel(tc, x_words, x_scales, mem, w1, slot, out_0, out_1, out_2):
@@ -131,7 +131,7 @@ def tile_picked_wkvput_none_lo_kernel(tc, x_words, x_scales, mem, w1, slot, out_
                 in_=grouped[:, PACK * c0 : PACK * c1],
             )
             nc.sync.dma_start(out=words_out[:, c0:c1], in_=out_codes[:, c0:c1].bitcast(I32))
-        for q in range(4):
-            nc.scalar.dma_start(
+        for q in (0, 2, 1, 3):
+            nc.sync.dma_start(
                 out=out_2[0, 4 * q : 4 * q + 4, :].bitcast(I32), in_=out_scales[32 * q : 32 * q + 4, :].bitcast(I32)
             )

@@ -13,13 +13,21 @@ U16 = mybir.dt.uint16
 U8 = mybir.dt.uint8
 FP8X4 = mybir.dt.float8_e4m3fn_x4
 FP4X4 = mybir.dt.float4_e2m1fn_x4
+MULT = mybir.AluOpType.mult
+ADD = mybir.AluOpType.add
 
 P = 128
 PACK = 4
 PASSES = K // (P * PACK)
 BANK = 512
 HALVES = T // BANK
-VECTOR_COLS = 1024
+SIDE = N // 2
+HP = P // 2
+EARLY = 640
+LATE = T - EARLY
+X_PIECES = ((0, EARLY), (BANK, T))
+SCALAR_COLS = 1088
+JOINT = 16
 VECTOR_PIECES = ((0, 512), (512, 1024))
 SCALAR_PIECES = ((1024, 1536), (1536, 1792), (1792, 2048))
 QUANT_PIECES = VECTOR_PIECES + SCALAR_PIECES
@@ -31,105 +39,156 @@ def tile_picked_wkvput_none_lo_kernel(tc, x_words, x_scales, mem, w1, slot, out_
         keep = ctx.enter_context(tc.tile_pool(name="keep", bufs=1))
         psum = ctx.enter_context(tc.psum_pool(name="psum", bufs=1))
 
+        def gpsimd_copy(out, in_):
+            nc.gpsimd.tensor_scalar(out=out, in0=in_, scalar1=1.0, scalar2=-0.0, op0=MULT, op1=ADD)
+
         offsets = keep.tile([P, T // 16], U16, name="offsets")
-        w_raw = [keep.tile([P, PACK, N], F32, name="w_raw%d" % g) for g in range(PASSES)]
-        w_bf = [keep.tile([P, PACK * N], BF16, name="w_bf%d" % g, align_bytes=64) for g in range(PASSES)]
-        w_codes = [keep.tile([P, N], U32, name="w_codes%d" % g, tag="codes%d" % g, align_bytes=64) for g in range(PASSES)]
-        w_scales = [keep.tile([P, N], U8, name="w_scales%d" % g, align_bytes=64) for g in range(PASSES)]
-        x_codes = [keep.tile([P, PASSES, 2 * BANK], U8, name="x_codes%d" % h, align_bytes=64) for h in range(HALVES)]
-        x_sc = [keep.tile([P, PASSES, BANK], U8, name="x_sc%d" % h, align_bytes=64) for h in range(HALVES)]
+        w_raw = [[keep.tile([P, PACK, SIDE], F32, name="w_raw%d_%d" % (s, g), tag="w_raw%d_%d" % (s, g)) for g in range(PASSES)] for s in range(2)]
+        even0_bf = [keep.tile([P, PACK * P], BF16, name="even0_bf%d" % g, align_bytes=64) for g in range(PASSES)]
+        even0_codes = [keep.tile([P, P], U32, name="even0_codes%d" % g, align_bytes=64) for g in range(PASSES)]
+        even0_scales = [keep.tile([P, P], U8, name="even0_scales%d" % g, align_bytes=64) for g in range(PASSES)]
+        even1_bf = keep.tile([P, PASSES * PACK * P], BF16, name="even1_bf", align_bytes=64)
+        even1_codes = keep.tile([P, PASSES * P], U32, name="even1_codes", align_bytes=64)
+        even1_scales = keep.tile([P, PASSES * P], U8, name="even1_scales", align_bytes=64)
+        odd_bf = [keep.tile([P, 2 * PACK * P], BF16, name="odd_bf%d" % g, align_bytes=64) for g in range(PASSES)]
+        odd_codes = [keep.tile([P, 2 * P], U32, name="odd_codes%d" % g, align_bytes=64) for g in range(PASSES)]
+        odd_scales = [keep.tile([P, 2 * P], U8, name="odd_scales%d" % g, align_bytes=64) for g in range(PASSES)]
+        x_codes = [keep.tile([P, PASSES, 2 * (j1 - j0)], U8, name="x_codes%d" % j0, align_bytes=64) for j0, j1 in X_PIECES]
+        x_sc = [keep.tile([P, PASSES, j1 - j0], U8, name="x_sc%d" % j0, align_bytes=64) for j0, j1 in X_PIECES]
         window = [keep.tile([P, U], F32, name="window%d" % t) for t in range(PACK)]
         y = [keep.tile([P, T], F32, name="y%d" % t) for t in range(PACK)]
+        moved = keep.tile([P, 2, U], BF16, name="moved")
+        grouped = keep.tile([P, U * PACK], BF16, name="grouped", align_bytes=64)
         out_codes = keep.tile([P, U], U32, name="out_codes", align_bytes=64)
         out_scales = keep.tile([P, U], U8, name="out_scales", align_bytes=64)
 
-        mem_rows = mem.rearrange("(p t) c -> p t c", t=PACK)
-        out_rows = out_0.rearrange("(p t) c -> p t c", t=PACK)
+        def rows_of(dram, t):
+            if t < 2:
+                return dram[SIDE * t : SIDE * (t + 1), :].rearrange("(p v) c -> p v c", v=2)[:, 0, :]
+            return dram.rearrange("(p r) c -> p r c", r=PACK)[:, 2 * (t - 2) + 1, :]
 
-        def load_w(g):
-            nc.sync.dma_start(out=w_raw[g][:], in_=w1[512 * g : 512 * (g + 1), :].rearrange("(p j) n -> p j n", j=PACK))
+        def load_w(s, g):
+            src = w1[512 * g : 512 * (g + 1), SIDE * s : SIDE * (s + 1)].rearrange("(p j) n -> p j n", j=PACK)
+            nc.sync.dma_start(out=w_raw[s][g][:], in_=src)
 
         def load_x(h):
+            j0, j1 = X_PIECES[h]
             for q in range(4):
-                rows = x_scales[:, 4 * q : 4 * q + 4, BANK * h : BANK * (h + 1)].rearrange("g r n -> r g n")
+                rows = x_scales[:, 4 * q : 4 * q + 4, j0:j1].rearrange("g r n -> r g n")
                 nc.sync.dma_start(out=x_sc[h][32 * q : 32 * q + 4, :, :].bitcast(I32), in_=rows.bitcast(I32))
-            src = x_words[:, :, 2 * BANK * h : 2 * BANK * (h + 1)].rearrange("g p n -> p g n")
+            src = x_words[:, :, 2 * j0 : 2 * j1].rearrange("g p n -> p g n")
             nc.sync.dma_start(out=x_codes[h][:].bitcast(I32), in_=src.bitcast(I32))
 
-        load_w(0)
-        load_w(1)
+        load_w(0, 0)
+        load_w(0, 1)
         load_x(0)
         nc.sync.dma_start(offsets[:], slot)
-        nc.sync.dma_start(out=window[0][:], in_=mem_rows[:, 0, :])
+        nc.sync.dma_start(out=window[0][:], in_=rows_of(mem, 0))
+        load_w(1, 0)
         load_x(1)
+        load_w(1, 1)
         for t in range(1, PACK):
-            nc.sync.dma_start(out=window[t][:], in_=mem_rows[:, t, :])
+            nc.sync.dma_start(out=window[t][:], in_=rows_of(mem, t))
 
-        def deal_w(copy, g, t0, t1):
-            dst = w_bf[g][:].rearrange("p (t m j) -> p m j t", t=PACK, j=PACK)
-            src = w_raw[g][:].rearrange("p j (m t) -> p m j t", t=PACK)
-            copy(out=dst[:, :, :, t0:t1], in_=src[:, :, :, t0:t1])
+        def deal_even(copy, dst, s, g):
+            src = w_raw[s][g][:].rearrange("p j (m v) -> p m j v", v=2)[:, :, :, 0]
+            copy(out=dst.rearrange("p (m j) -> p m j", j=PACK), in_=src)
 
-        def quantize_w(g, t0, t1):
-            nc.vector.quantize_mx(
-                out=w_codes[g][:, P * t0 : P * t1].bitcast(FP8X4),
-                scales=w_scales[g][:, P * t0 : P * t1],
-                in_=w_bf[g][:, PACK * P * t0 : PACK * P * t1],
-            )
+        def deal_odd(copy, s, g):
+            dst = odd_bf[g][:].rearrange("p (u s m j) -> p s m j u", u=2, s=2, j=PACK)[:, s]
+            src = w_raw[s][g][:].rearrange("p j (m u v) -> p v m j u", u=2, v=2)[:, 1]
+            copy(out=dst, in_=src)
+
+        def quantize(codes, scales, values, c0, c1):
+            nc.vector.quantize_mx(out=codes[:, c0:c1].bitcast(FP8X4), scales=scales[:, c0:c1], in_=values[:, PACK * c0 : PACK * c1])
+
+        def quantize_odd(s, g):
+            for u in range(2):
+                quantize(odd_codes[g], odd_scales[g], odd_bf[g], P * u + HP * s, P * u + HP * (s + 1))
 
         for g in range(PASSES):
-            deal_w(nc.vector.tensor_copy, g, 0, 2)
-            deal_w(nc.scalar.copy, g, 2, 4)
-            quantize_w(g, 0, 2)
-            quantize_w(g, 2, 4)
+            deal_even(nc.vector.tensor_copy, even0_bf[g][:], 0, g)
+            deal_odd(nc.vector.tensor_copy, 0, g)
+            quantize(even0_codes[g], even0_scales[g], even0_bf[g], 0, P)
+            quantize_odd(0, g)
+        def weights_of(t, g):
+            if t == 0:
+                return even0_codes[g][:], even0_scales[g][:]
+            if t == 1:
+                return even1_codes[:, P * g : P * (g + 1)], even1_scales[:, P * g : P * (g + 1)]
+            return odd_codes[g][:, P * (t - 2) : P * (t - 1)], odd_scales[g][:, P * (t - 2) : P * (t - 1)]
 
-        for t in range(PACK):
-            for h in range(HALVES):
-                acc = psum.tile([P, BANK], F32, name="acc%d_%d" % (t, h))
-                for g in range(PASSES):
+        def product(t, h, j0, width, bank, tag):
+            acc = psum.tile([P, bank], F32, name="acc%d_%d" % (t, j0), tag=tag)
+            order = range(PASSES) if t < 2 else range(PASSES - 1, -1, -1)
+            for c0 in range(0, bank, width):
+                x0 = j0 + c0 - X_PIECES[h][0]
+                for g in order:
+                    codes, scales = weights_of(t, g)
                     nc.tensor.matmul_mx(
-                        out=acc[:],
-                        lhsT=w_codes[g][:, P * t : P * (t + 1)].bitcast(FP8X4),
-                        lhsT_scale=w_scales[g][:, P * t : P * (t + 1)],
-                        rhs=x_codes[h][:, g, :].bitcast(FP4X4),
-                        rhs_scale=x_sc[h][:, g, :],
-                        start=(g == 0),
-                        stop=(g == PASSES - 1),
+                        out=acc[:, c0 : c0 + width],
+                        lhsT=codes.bitcast(FP8X4),
+                        lhsT_scale=scales,
+                        rhs=x_codes[h][:, g, 2 * x0 : 2 * (x0 + width)].bitcast(FP4X4),
+                        rhs_scale=x_sc[h][:, g, x0 : x0 + width],
+                        start=(g == order[0]),
+                        stop=(g == order[-1]),
                     )
+            return acc
+
+        nc.scalar.copy(out=y[0][:, 0:BANK], in_=product(0, 0, 0, BANK, BANK, "bank0")[:])
+        nc.scalar.copy(out=y[0][:, BANK:EARLY], in_=product(0, 0, BANK, P, EARLY - BANK, "bank1")[:])
+        for g in range(PASSES):
+            deal_even(nc.scalar.copy, even1_bf[:, PACK * P * g : PACK * P * (g + 1)], 1, g)
+            deal_odd(nc.scalar.copy, 1, g)
+        quantize_odd(1, 0)
+        quantize(even1_codes, even1_scales, even1_bf, 0, PASSES * P)
+        quantize_odd(1, 1)
+        y_late = keep.tile([P, LATE], F32, name="y_late", tag="w_raw1_1")
+        nc.scalar.copy(out=y_late[:], in_=product(0, 1, EARLY, P, LATE, "bank0")[:])
+        for t in range(1, PACK):
+            for h in range(HALVES):
+                acc = product(t, h, BANK * h, BANK, BANK, "bank%d" % (2 * t + h))
                 nc.scalar.copy(out=y[t][:, BANK * h : BANK * (h + 1)], in_=acc[:])
 
-        grouped = keep.tile([P, U * PACK], BF16, name="grouped", tag="codes1", align_bytes=64)
-        by_col = grouped[:].rearrange("p (c t) -> p c t", t=PACK)
+        rounded = keep.tile([P, U], BF16, name="rounded")
+        by_col = grouped[:].rearrange("p (c u d) -> p c u d", u=2, d=2)
+        shares = ((nc.scalar.copy, 0, SCALAR_COLS), (gpsimd_copy, SCALAR_COLS, U))
+
+        def scatter(t, values, j0, j1):
+            nc.vector.tensor_copy(window[t][:].indirect(offsets[:, j0 // 16 : j1 // 16]), values)
 
         for t in range(PACK):
             if t == 0:
-                for h in range(HALVES):
-                    cols = BANK // 16
-                    nc.vector.tensor_copy(
-                        window[t][:].indirect(offsets[:, cols * h : cols * (h + 1)]), y[t][:, BANK * h : BANK * (h + 1)]
-                    )
+                scatter(t, y[t][:, 0:EARLY], 0, EARLY)
+                scatter(t, y_late[:], EARLY, T)
+            elif t == 1:
+                scatter(t, y[t][:, 0:BANK], 0, BANK)
+                scatter(t, y[t][:, BANK:T], BANK, T)
             else:
-                nc.vector.tensor_copy(window[t][:].indirect(offsets[:]), y[t][:])
-            nc.sync.dma_start(out=out_rows[:, t, :], in_=window[t][:])
+                scatter(t, y[t][:], 0, T)
+            nc.sync.dma_start(out=rows_of(out_0, t), in_=window[t][:])
             if t < 2:
-                nc.scalar.copy(out=by_col[:, :, t], in_=window[t][:])
+                for copy, c0, c1 in shares if t == 1 else ((gpsimd_copy, 0, U),):
+                    copy(out=rounded[:, c0:c1], in_=window[t][:, c0:c1])
+                for u in range(2):
+                    nc.scalar.dma_start(out=moved[HP * t : HP * (t + 1), u, :], in_=rounded[u:P:2, :])
             elif t == 2:
-                twice = window[t][:, 0:VECTOR_COLS].unsqueeze(2).to_broadcast([P, VECTOR_COLS, 2])
-                nc.scalar.copy(out=by_col[:, 0:VECTOR_COLS, 2:4], in_=twice)
-                nc.scalar.copy(out=by_col[:, VECTOR_COLS:U, 2], in_=window[t][:, VECTOR_COLS:U])
+                pairs = moved[:].rearrange("p u c -> p c u")
+                for copy, c0, c1 in shares:
+                    cj = c1 - JOINT
+                    copy(out=by_col[:, c0:cj, :, 0], in_=pairs[:, c0:cj, :])
+                    copy(out=by_col[:, cj:c1, :, :], in_=pairs[:, cj:c1, :].unsqueeze(3).to_broadcast([P, JOINT, 2, 2]))
+                    copy(out=by_col[:, c0:c1, :, 1], in_=window[t][:, c0:c1].unsqueeze(2).to_broadcast([P, c1 - c0, 2]))
 
         last = PACK - 1
         for c0, c1 in VECTOR_PIECES:
-            nc.vector.tensor_copy(out=by_col[:, c0:c1, last], in_=window[last][:, c0:c1])
+            nc.vector.tensor_copy(out=by_col[:, c0:c1, 1, 1], in_=window[last][:, c0:c1])
         for c0, c1 in SCALAR_PIECES:
-            nc.scalar.copy(out=by_col[:, c0:c1, last], in_=window[last][:, c0:c1])
+            nc.scalar.copy(out=by_col[:, c0:c1, 1, 1], in_=window[last][:, c0:c1])
         words_out = out_1[0].rearrange("p c r -> p (c r)").bitcast(I32)
         for c0, c1 in QUANT_PIECES:
-            nc.vector.quantize_mx(
-                out=out_codes[:, c0:c1].bitcast(FP8X4),
-                scales=out_scales[:, c0:c1],
-                in_=grouped[:, PACK * c0 : PACK * c1],
-            )
+            quantize(out_codes, out_scales, grouped, c0, c1)
             nc.sync.dma_start(out=words_out[:, c0:c1], in_=out_codes[:, c0:c1].bitcast(I32))
         for q in (0, 2, 1, 3):
             nc.sync.dma_start(

@@ -27,6 +27,8 @@ EARLY = 640
 LATE = T - EARLY
 X_PIECES = ((0, EARLY), (BANK, T))
 SCALAR_COLS = 1088
+PAIR_SPLIT = 384
+THIRD_SPLIT = 1536
 JOINT = 16
 VECTOR_PIECES = ((0, 512), (512, 1024))
 SCALAR_PIECES = ((1024, 1536), (1536, 1792), (1792, 2048))
@@ -64,8 +66,8 @@ def tile_picked_wkvput_none_lo_kernel(tc, x_words, x_scales, mem, w1, slot, out_
 
         def rows_of(dram, t):
             if t < 2:
-                return dram[SIDE * t : SIDE * (t + 1), :].rearrange("(p v) c -> p v c", v=2)[:, 0, :]
-            return dram.rearrange("(p r) c -> p r c", r=PACK)[:, 2 * (t - 2) + 1, :]
+                return dram[SIDE * t : SIDE * (t + 1), :].rearrange("(l r) c -> l r c", r=PACK)[:, 0:2, :]
+            return dram.rearrange("(p r) c -> p r c", r=PACK)[:, t, :]
 
         def load_w(s, g):
             src = w1[512 * g : 512 * (g + 1), SIDE * s : SIDE * (s + 1)].rearrange("(p j) n -> p j n", j=PACK)
@@ -91,12 +93,12 @@ def tile_picked_wkvput_none_lo_kernel(tc, x_words, x_scales, mem, w1, slot, out_
             nc.sync.dma_start(out=window[t][:], in_=rows_of(mem, t))
 
         def deal_even(copy, dst, s, g):
-            src = w_raw[s][g][:].rearrange("p j (m v) -> p m j v", v=2)[:, :, :, 0]
-            copy(out=dst.rearrange("p (m j) -> p m j", j=PACK), in_=src)
+            src = w_raw[s][g][:].rearrange("p j (l r) -> p l j r", r=PACK)[:, :, :, 0:2]
+            copy(out=dst.rearrange("p (l v j) -> p l j v", v=2, j=PACK), in_=src)
 
         def deal_odd(copy, s, g):
             dst = odd_bf[g][:].rearrange("p (u s m j) -> p s m j u", u=2, s=2, j=PACK)[:, s]
-            src = w_raw[s][g][:].rearrange("p j (m u v) -> p v m j u", u=2, v=2)[:, 1]
+            src = w_raw[s][g][:].rearrange("p j (l r) -> p l j r", r=PACK)[:, :, :, 2:4]
             copy(out=dst, in_=src)
 
         def quantize(codes, scales, values, c0, c1):
@@ -152,7 +154,7 @@ def tile_picked_wkvput_none_lo_kernel(tc, x_words, x_scales, mem, w1, slot, out_
                 nc.scalar.copy(out=y[t][:, BANK * h : BANK * (h + 1)], in_=acc[:])
 
         rounded = keep.tile([P, U], BF16, name="rounded")
-        by_col = grouped[:].rearrange("p (c u d) -> p c u d", u=2, d=2)
+        by_col = grouped[:].rearrange("p (c d v) -> p c d v", d=2, v=2)
         shares = ((nc.scalar.copy, 0, SCALAR_COLS), (gpsimd_copy, SCALAR_COLS, U))
 
         def scatter(t, values, j0, j1):
@@ -171,15 +173,15 @@ def tile_picked_wkvput_none_lo_kernel(tc, x_words, x_scales, mem, w1, slot, out_
             if t < 2:
                 for copy, c0, c1 in shares if t == 1 else ((gpsimd_copy, 0, U),):
                     copy(out=rounded[:, c0:c1], in_=window[t][:, c0:c1])
-                for u in range(2):
-                    nc.scalar.dma_start(out=moved[HP * t : HP * (t + 1), u, :], in_=rounded[u:P:2, :])
+                nc.scalar.dma_start(out=moved[HP * t : HP * (t + 1), :, :], in_=rounded[:])
             elif t == 2:
-                pairs = moved[:].rearrange("p u c -> p c u")
-                for copy, c0, c1 in shares:
+                pairs = moved[:].rearrange("p v c -> p c v")
+                for copy, c0, c1 in ((gpsimd_copy, 0, PAIR_SPLIT), (nc.scalar.copy, PAIR_SPLIT, U)):
                     cj = c1 - JOINT
-                    copy(out=by_col[:, c0:cj, :, 0], in_=pairs[:, c0:cj, :])
-                    copy(out=by_col[:, cj:c1, :, :], in_=pairs[:, cj:c1, :].unsqueeze(3).to_broadcast([P, JOINT, 2, 2]))
-                    copy(out=by_col[:, c0:c1, :, 1], in_=window[t][:, c0:c1].unsqueeze(2).to_broadcast([P, c1 - c0, 2]))
+                    copy(out=by_col[:, c0:cj, 0, :], in_=pairs[:, c0:cj, :])
+                    copy(out=by_col[:, cj:c1, :, :], in_=pairs[:, cj:c1, :].unsqueeze(2).to_broadcast([P, JOINT, 2, 2]))
+                for copy, c0, c1 in ((gpsimd_copy, 0, THIRD_SPLIT), (nc.scalar.copy, THIRD_SPLIT, U)):
+                    copy(out=by_col[:, c0:c1, 1, :], in_=window[t][:, c0:c1].unsqueeze(2).to_broadcast([P, c1 - c0, 2]))
 
         last = PACK - 1
         for c0, c1 in VECTOR_PIECES:

@@ -26,9 +26,8 @@ HP = P // 2
 EARLY = 640
 LATE = T - EARLY
 X_PIECES = ((0, EARLY), (BANK, T))
-SCALAR_COLS = 1088
-PAIR_SPLIT = 384
-THIRD_SPLIT = 1536
+MOVE_PIECES = ((0, 1024), (1024, 2048))
+THIRD_SCALAR = (1504, 1824)
 JOINT = 16
 VECTOR_PIECES = ((0, 512), (512, 1024))
 SCALAR_PIECES = ((1024, 1536), (1536, 1792), (1792, 2048))
@@ -59,7 +58,7 @@ def tile_picked_wkvput_none_lo_kernel(tc, x_words, x_scales, mem, w1, slot, out_
         x_sc = [keep.tile([P, PASSES, j1 - j0], U8, name="x_sc%d" % j0, align_bytes=64) for j0, j1 in X_PIECES]
         window = [keep.tile([P, U], F32, name="window%d" % t) for t in range(PACK)]
         y = [keep.tile([P, T], F32, name="y%d" % t) for t in range(PACK)]
-        moved = keep.tile([P, 2, U], BF16, name="moved")
+        moved = {c0: keep.tile([P, 2, c1 - c0], BF16, name="moved%d" % c0) for c0, c1 in MOVE_PIECES}
         grouped = keep.tile([P, U * PACK], BF16, name="grouped", align_bytes=64)
         out_codes = keep.tile([P, U], U32, name="out_codes", align_bytes=64)
         out_scales = keep.tile([P, U], U8, name="out_scales", align_bytes=64)
@@ -155,7 +154,10 @@ def tile_picked_wkvput_none_lo_kernel(tc, x_words, x_scales, mem, w1, slot, out_
 
         rounded = keep.tile([P, U], BF16, name="rounded")
         by_col = grouped[:].rearrange("p (c d v) -> p c d v", d=2, v=2)
-        shares = ((nc.scalar.copy, 0, SCALAR_COLS), (gpsimd_copy, SCALAR_COLS, U))
+
+        def pairs_of(c0, c1):
+            base = c0 - c0 % (U // 2)
+            return moved[base][:].rearrange("p v c -> p c v")[:, c0 - base : c1 - base, :]
 
         def scatter(t, values, j0, j1):
             nc.vector.tensor_copy(window[t][:].indirect(offsets[:, j0 // 16 : j1 // 16]), values)
@@ -171,16 +173,17 @@ def tile_picked_wkvput_none_lo_kernel(tc, x_words, x_scales, mem, w1, slot, out_
                 scatter(t, y[t][:], 0, T)
             nc.sync.dma_start(out=rows_of(out_0, t), in_=window[t][:])
             if t < 2:
-                for copy, c0, c1 in shares if t == 1 else ((gpsimd_copy, 0, U),):
+                copy = gpsimd_copy if t == 0 else nc.scalar.copy
+                for c0, c1 in MOVE_PIECES:
                     copy(out=rounded[:, c0:c1], in_=window[t][:, c0:c1])
-                nc.scalar.dma_start(out=moved[HP * t : HP * (t + 1), :, :], in_=rounded[:])
+                    nc.scalar.dma_start(out=moved[c0][HP * t : HP * (t + 1), :, :], in_=rounded[:, c0:c1])
             elif t == 2:
-                pairs = moved[:].rearrange("p v c -> p c v")
-                for copy, c0, c1 in ((gpsimd_copy, 0, PAIR_SPLIT), (nc.scalar.copy, PAIR_SPLIT, U)):
-                    cj = c1 - JOINT
-                    copy(out=by_col[:, c0:cj, 0, :], in_=pairs[:, c0:cj, :])
-                    copy(out=by_col[:, cj:c1, :, :], in_=pairs[:, cj:c1, :].unsqueeze(2).to_broadcast([P, JOINT, 2, 2]))
-                for copy, c0, c1 in ((gpsimd_copy, 0, THIRD_SPLIT), (nc.scalar.copy, THIRD_SPLIT, U)):
+                s0, s1 = THIRD_SCALAR
+                for c0, c1 in ((0, U // 2), (U // 2, s1 - JOINT), (s1, U)):
+                    nc.scalar.copy(out=by_col[:, c0:c1, 0, :], in_=pairs_of(c0, c1))
+                joint = pairs_of(s1 - JOINT, s1).unsqueeze(2).to_broadcast([P, JOINT, 2, 2])
+                nc.scalar.copy(out=by_col[:, s1 - JOINT : s1, :, :], in_=joint)
+                for copy, c0, c1 in ((gpsimd_copy, 0, s0), (gpsimd_copy, s1, U), (nc.scalar.copy, s0, s1)):
                     copy(out=by_col[:, c0:c1, 1, :], in_=window[t][:, c0:c1].unsqueeze(2).to_broadcast([P, c1 - c0, 2]))
 
         last = PACK - 1

@@ -26,8 +26,10 @@ HP = P // 2
 EARLY = 640
 LATE = T - EARLY
 X_PIECES = ((0, EARLY), (BANK, T))
-MOVE_PIECES = ((0, 1024), (1024, 2048))
-THIRD_SCALAR = (1504, 1824)
+FIRST_MOVE = 640
+MOVE_PIECES = ((0, FIRST_MOVE), (FIRST_MOVE, U))
+PAIR_SPLIT = 1024
+THIRD_SPLIT = 704
 JOINT = 16
 VECTOR_PIECES = ((0, 512), (512, 1024))
 SCALAR_PIECES = ((1024, 1536), (1536, 1792), (1792, 2048))
@@ -52,7 +54,7 @@ def tile_picked_wkvput_none_lo_kernel(tc, x_words, x_scales, mem, w1, slot, out_
         even1_codes = keep.tile([P, PASSES * P], U32, name="even1_codes", align_bytes=64)
         even1_scales = keep.tile([P, PASSES * P], U8, name="even1_scales", align_bytes=64)
         odd_bf = [keep.tile([P, 2 * PACK * P], BF16, name="odd_bf%d" % g, align_bytes=64) for g in range(PASSES)]
-        odd_codes = [keep.tile([P, 2 * P], U32, name="odd_codes%d" % g, align_bytes=64) for g in range(PASSES)]
+        odd_codes = [keep.tile([P, 2 * P], U32, name="odd_codes%d" % g, tag="odd%d" % (1 - g), align_bytes=64) for g in range(PASSES)]
         odd_scales = [keep.tile([P, 2 * P], U8, name="odd_scales%d" % g, align_bytes=64) for g in range(PASSES)]
         x_codes = [keep.tile([P, PASSES, 2 * (j1 - j0)], U8, name="x_codes%d" % j0, align_bytes=64) for j0, j1 in X_PIECES]
         x_sc = [keep.tile([P, PASSES, j1 - j0], U8, name="x_sc%d" % j0, align_bytes=64) for j0, j1 in X_PIECES]
@@ -153,10 +155,11 @@ def tile_picked_wkvput_none_lo_kernel(tc, x_words, x_scales, mem, w1, slot, out_
                 nc.scalar.copy(out=y[t][:, BANK * h : BANK * (h + 1)], in_=acc[:])
 
         rounded = keep.tile([P, U], BF16, name="rounded")
+        rounded_first = keep.tile([P, FIRST_MOVE], BF16, name="rounded_first", tag="odd1", align_bytes=64)
         by_col = grouped[:].rearrange("p (c d v) -> p c d v", d=2, v=2)
 
         def pairs_of(c0, c1):
-            base = c0 - c0 % (U // 2)
+            base = 0 if c0 < FIRST_MOVE else FIRST_MOVE
             return moved[base][:].rearrange("p v c -> p c v")[:, c0 - base : c1 - base, :]
 
         def scatter(t, values, j0, j1):
@@ -173,18 +176,22 @@ def tile_picked_wkvput_none_lo_kernel(tc, x_words, x_scales, mem, w1, slot, out_
                 scatter(t, y[t][:], 0, T)
             nc.sync.dma_start(out=rows_of(out_0, t), in_=window[t][:])
             if t < 2:
-                copy = gpsimd_copy if t == 0 else nc.scalar.copy
-                for c0, c1 in MOVE_PIECES:
-                    copy(out=rounded[:, c0:c1], in_=window[t][:, c0:c1])
-                    nc.scalar.dma_start(out=moved[c0][HP * t : HP * (t + 1), :, :], in_=rounded[:, c0:c1])
+                if t == 0:
+                    gpsimd_copy(out=rounded[:], in_=window[t][:])
+                for c0, c1 in MOVE_PIECES if t == 1 else reversed(MOVE_PIECES):
+                    staged = rounded_first[:] if t == 1 and c0 == 0 else rounded[:, c0:c1]
+                    if t == 1:
+                        nc.scalar.copy(out=staged, in_=window[t][:, c0:c1])
+                    nc.scalar.dma_start(out=moved[c0][HP * t : HP * (t + 1), :, :], in_=staged)
             elif t == 2:
-                s0, s1 = THIRD_SCALAR
-                for c0, c1 in ((0, U // 2), (U // 2, s1 - JOINT), (s1, U)):
+                cj = PAIR_SPLIT - JOINT
+                for c0, c1 in ((0, FIRST_MOVE), (FIRST_MOVE, cj)):
                     nc.scalar.copy(out=by_col[:, c0:c1, 0, :], in_=pairs_of(c0, c1))
-                joint = pairs_of(s1 - JOINT, s1).unsqueeze(2).to_broadcast([P, JOINT, 2, 2])
-                nc.scalar.copy(out=by_col[:, s1 - JOINT : s1, :, :], in_=joint)
-                for copy, c0, c1 in ((gpsimd_copy, 0, s0), (gpsimd_copy, s1, U), (nc.scalar.copy, s0, s1)):
+                joint = pairs_of(cj, PAIR_SPLIT).unsqueeze(2).to_broadcast([P, JOINT, 2, 2])
+                nc.scalar.copy(out=by_col[:, cj:PAIR_SPLIT, :, :], in_=joint)
+                for copy, c0, c1 in ((gpsimd_copy, 0, THIRD_SPLIT), (nc.scalar.copy, THIRD_SPLIT, U)):
                     copy(out=by_col[:, c0:c1, 1, :], in_=window[t][:, c0:c1].unsqueeze(2).to_broadcast([P, c1 - c0, 2]))
+                gpsimd_copy(out=by_col[:, PAIR_SPLIT:U, 0, :], in_=pairs_of(PAIR_SPLIT, U))
 
         last = PACK - 1
         for c0, c1 in VECTOR_PIECES:

@@ -13,27 +13,26 @@ U16 = mybir.dt.uint16
 U8 = mybir.dt.uint8
 FP8X4 = mybir.dt.float8_e4m3fn_x4
 FP4X4 = mybir.dt.float4_e2m1fn_x4
-MULT = mybir.AluOpType.mult
-ADD = mybir.AluOpType.add
 
 P = 128
 PACK = 4
 PASSES = K // (P * PACK)
 BANK = 512
-HALVES = T // BANK
+LIST_ROWS = 16
 SIDE = N // 2
-HP = P // 2
+HALF_P = P // 2
+
 EARLY = 640
 LATE = T - EARLY
 X_PIECES = ((0, EARLY), (BANK, T))
-FIRST_MOVE = 640
-MOVE_PIECES = ((0, FIRST_MOVE), (FIRST_MOVE, U))
-PAIR_SPLIT = 1024
-THIRD_SPLIT = 704
+FIRST_MOVE = 512
+MOVE_PIECES = ((0, FIRST_MOVE), (FIRST_MOVE, 1024), (1024, U))
+THIRD_SPLIT = 1776
+RUN = 4
 JOINT = 16
 VECTOR_PIECES = ((0, 512), (512, 1024))
-SCALAR_PIECES = ((1024, 1536), (1536, 1792), (1792, 2048))
-QUANT_PIECES = VECTOR_PIECES + SCALAR_PIECES
+SCALAR_PIECES = ((1024, 1792), (1792, 2048))
+QUANT_PIECES = VECTOR_PIECES + ((1024, 1536), (1536, 1792), (1792, 2048))
 
 
 def tile_picked_wkvput_none_lo_kernel(tc, x_words, x_scales, mem, w1, slot, out_0, out_1, out_2):
@@ -43,19 +42,26 @@ def tile_picked_wkvput_none_lo_kernel(tc, x_words, x_scales, mem, w1, slot, out_
         psum = ctx.enter_context(tc.psum_pool(name="psum", bufs=1))
 
         def gpsimd_copy(out, in_):
-            nc.gpsimd.tensor_scalar(out=out, in0=in_, scalar1=1.0, scalar2=-0.0, op0=MULT, op1=ADD)
+            nc.gpsimd.tensor_scalar(
+                out=out, in0=in_, scalar1=1.0, scalar2=-0.0, op0=mybir.AluOpType.mult, op1=mybir.AluOpType.add
+            )
 
-        offsets = keep.tile([P, T // 16], U16, name="offsets")
-        w_raw = [[keep.tile([P, PACK, SIDE], F32, name="w_raw%d_%d" % (s, g), tag="w_raw%d_%d" % (s, g)) for g in range(PASSES)] for s in range(2)]
-        even0_bf = [keep.tile([P, PACK * P], BF16, name="even0_bf%d" % g, align_bytes=64) for g in range(PASSES)]
-        even0_codes = [keep.tile([P, P], U32, name="even0_codes%d" % g, align_bytes=64) for g in range(PASSES)]
-        even0_scales = [keep.tile([P, P], U8, name="even0_scales%d" % g, align_bytes=64) for g in range(PASSES)]
-        even1_bf = keep.tile([P, PASSES * PACK * P], BF16, name="even1_bf", align_bytes=64)
-        even1_codes = keep.tile([P, PASSES * P], U32, name="even1_codes", align_bytes=64)
-        even1_scales = keep.tile([P, PASSES * P], U8, name="even1_scales", align_bytes=64)
-        odd_bf = [keep.tile([P, 2 * PACK * P], BF16, name="odd_bf%d" % g, align_bytes=64) for g in range(PASSES)]
-        odd_codes = [keep.tile([P, 2 * P], U32, name="odd_codes%d" % g, tag="odd%d" % (1 - g), align_bytes=64) for g in range(PASSES)]
-        odd_scales = [keep.tile([P, 2 * P], U8, name="odd_scales%d" % g, align_bytes=64) for g in range(PASSES)]
+        offsets = keep.tile([P, T // LIST_ROWS], U16, name="offsets")
+        w_raw = [
+            [keep.tile([P, PACK, SIDE], F32, name="w_raw%d_%d" % (s, g), tag="w_raw%d_%d" % (s, g)) for g in range(PASSES)]
+            for s in range(2)
+        ]
+        w0_bf = [keep.tile([P, PACK * P], BF16, name="w0_bf%d" % g, align_bytes=64) for g in range(PASSES)]
+        w0_codes = [keep.tile([P, P], U32, name="w0_codes%d" % g, align_bytes=64) for g in range(PASSES)]
+        w0_scales = [keep.tile([P, P], U8, name="w0_scales%d" % g, align_bytes=64) for g in range(PASSES)]
+        w1st_bf = keep.tile([P, PASSES * PACK * P], BF16, name="w1st_bf", align_bytes=64)
+        w1st_codes = keep.tile([P, PASSES * P], U32, name="w1st_codes", tag="w1st_codes", align_bytes=64)
+        w1st_scales = keep.tile([P, PASSES * P], U8, name="w1st_scales", align_bytes=64)
+        w23_bf = [keep.tile([P, 2 * PACK * P], BF16, name="w23_bf%d" % g, align_bytes=64) for g in range(PASSES)]
+        w23_codes = [
+            keep.tile([P, 2 * P], U32, name="w23_codes%d" % g, tag="w23_codes%d" % g, align_bytes=64) for g in range(PASSES)
+        ]
+        w23_scales = [keep.tile([P, 2 * P], U8, name="w23_scales%d" % g, align_bytes=64) for g in range(PASSES)]
         x_codes = [keep.tile([P, PASSES, 2 * (j1 - j0)], U8, name="x_codes%d" % j0, align_bytes=64) for j0, j1 in X_PIECES]
         x_sc = [keep.tile([P, PASSES, j1 - j0], U8, name="x_sc%d" % j0, align_bytes=64) for j0, j1 in X_PIECES]
         window = [keep.tile([P, U], F32, name="window%d" % t) for t in range(PACK)]
@@ -71,60 +77,55 @@ def tile_picked_wkvput_none_lo_kernel(tc, x_words, x_scales, mem, w1, slot, out_
             return dram.rearrange("(p r) c -> p r c", r=PACK)[:, t, :]
 
         def load_w(s, g):
-            src = w1[512 * g : 512 * (g + 1), SIDE * s : SIDE * (s + 1)].rearrange("(p j) n -> p j n", j=PACK)
-            nc.sync.dma_start(out=w_raw[s][g][:], in_=src)
+            rows = w1[P * PACK * g : P * PACK * (g + 1), SIDE * s : SIDE * (s + 1)]
+            nc.sync.dma_start(out=w_raw[s][g][:], in_=rows.rearrange("(p j) n -> p j n", j=PACK))
 
         def load_x(h):
             j0, j1 = X_PIECES[h]
             for q in range(4):
                 rows = x_scales[:, 4 * q : 4 * q + 4, j0:j1].rearrange("g r n -> r g n")
                 nc.sync.dma_start(out=x_sc[h][32 * q : 32 * q + 4, :, :].bitcast(I32), in_=rows.bitcast(I32))
-            src = x_words[:, :, 2 * j0 : 2 * j1].rearrange("g p n -> p g n")
-            nc.sync.dma_start(out=x_codes[h][:].bitcast(I32), in_=src.bitcast(I32))
+            words = x_words[:, :, 2 * j0 : 2 * j1].rearrange("g p n -> p g n")
+            nc.sync.dma_start(out=x_codes[h][:].bitcast(I32), in_=words.bitcast(I32))
 
         load_w(0, 0)
         load_w(0, 1)
         load_x(0)
-        nc.sync.dma_start(offsets[:], slot)
         nc.sync.dma_start(out=window[0][:], in_=rows_of(mem, 0))
+        nc.sync.dma_start(offsets[:], slot)
         load_w(1, 0)
         load_x(1)
         load_w(1, 1)
         for t in range(1, PACK):
             nc.sync.dma_start(out=window[t][:], in_=rows_of(mem, t))
 
-        def deal_even(copy, dst, s, g):
+        def deal_pairs(copy, dst, s, g):
             src = w_raw[s][g][:].rearrange("p j (l r) -> p l j r", r=PACK)[:, :, :, 0:2]
             copy(out=dst.rearrange("p (l v j) -> p l j v", v=2, j=PACK), in_=src)
 
-        def deal_odd(copy, s, g):
-            dst = odd_bf[g][:].rearrange("p (u s m j) -> p s m j u", u=2, s=2, j=PACK)[:, s]
+        def deal_23(copy, s, g):
+            dst = w23_bf[g][:].rearrange("p (u s l j) -> p s l j u", u=2, s=2, j=PACK)[:, s]
             src = w_raw[s][g][:].rearrange("p j (l r) -> p l j r", r=PACK)[:, :, :, 2:4]
             copy(out=dst, in_=src)
 
         def quantize(codes, scales, values, c0, c1):
             nc.vector.quantize_mx(out=codes[:, c0:c1].bitcast(FP8X4), scales=scales[:, c0:c1], in_=values[:, PACK * c0 : PACK * c1])
 
-        def quantize_odd(s, g):
+        def quantize_23(s, g):
             for u in range(2):
-                quantize(odd_codes[g], odd_scales[g], odd_bf[g], P * u + HP * s, P * u + HP * (s + 1))
+                quantize(w23_codes[g], w23_scales[g], w23_bf[g], P * u + HALF_P * s, P * u + HALF_P * (s + 1))
 
-        for g in range(PASSES):
-            deal_even(nc.vector.tensor_copy, even0_bf[g][:], 0, g)
-            deal_odd(nc.vector.tensor_copy, 0, g)
-            quantize(even0_codes[g], even0_scales[g], even0_bf[g], 0, P)
-            quantize_odd(0, g)
         def weights_of(t, g):
             if t == 0:
-                return even0_codes[g][:], even0_scales[g][:]
+                return w0_codes[g][:], w0_scales[g][:]
             if t == 1:
-                return even1_codes[:, P * g : P * (g + 1)], even1_scales[:, P * g : P * (g + 1)]
-            return odd_codes[g][:, P * (t - 2) : P * (t - 1)], odd_scales[g][:, P * (t - 2) : P * (t - 1)]
+                return w1st_codes[:, P * g : P * (g + 1)], w1st_scales[:, P * g : P * (g + 1)]
+            return w23_codes[g][:, P * (t - 2) : P * (t - 1)], w23_scales[g][:, P * (t - 2) : P * (t - 1)]
 
-        def product(t, h, j0, width, bank, tag):
-            acc = psum.tile([P, bank], F32, name="acc%d_%d" % (t, j0), tag=tag)
+        def product(t, h, j0, j1, width, bank):
+            acc = psum.tile([P, j1 - j0], F32, name="acc%d_%d" % (t, j0), tag="bank%d" % bank)
             order = range(PASSES) if t < 2 else range(PASSES - 1, -1, -1)
-            for c0 in range(0, bank, width):
+            for c0 in range(0, j1 - j0, width):
                 x0 = j0 + c0 - X_PIECES[h][0]
                 for g in order:
                     codes, scales = weights_of(t, g)
@@ -139,65 +140,74 @@ def tile_picked_wkvput_none_lo_kernel(tc, x_words, x_scales, mem, w1, slot, out_
                     )
             return acc
 
-        nc.scalar.copy(out=y[0][:, 0:BANK], in_=product(0, 0, 0, BANK, BANK, "bank0")[:])
-        nc.scalar.copy(out=y[0][:, BANK:EARLY], in_=product(0, 0, BANK, P, EARLY - BANK, "bank1")[:])
         for g in range(PASSES):
-            deal_even(nc.scalar.copy, even1_bf[:, PACK * P * g : PACK * P * (g + 1)], 1, g)
-            deal_odd(nc.scalar.copy, 1, g)
-        quantize_odd(1, 0)
-        quantize(even1_codes, even1_scales, even1_bf, 0, PASSES * P)
-        quantize_odd(1, 1)
+            deal_pairs(nc.vector.tensor_copy, w0_bf[g][:], 0, g)
+            deal_23(nc.vector.tensor_copy, 0, g)
+            quantize(w0_codes[g], w0_scales[g], w0_bf[g], 0, P)
+            quantize_23(0, g)
+        nc.scalar.copy(out=y[0][:, 0:BANK], in_=product(0, 0, 0, BANK, BANK, 0)[:])
+        nc.vector.tensor_copy(out=y[0][:, BANK:EARLY], in_=product(0, 0, BANK, EARLY, P, 1)[:])
+
+        for g in range(PASSES):
+            deal_pairs(nc.scalar.copy, w1st_bf[:, PACK * P * g : PACK * P * (g + 1)], 1, g)
+            deal_23(nc.scalar.copy, 1, g)
+        quantize_23(1, 0)
+        quantize(w1st_codes, w1st_scales, w1st_bf, 0, PASSES * P)
+        quantize_23(1, 1)
         y_late = keep.tile([P, LATE], F32, name="y_late", tag="w_raw1_1")
-        nc.scalar.copy(out=y_late[:], in_=product(0, 1, EARLY, P, LATE, "bank0")[:])
+        nc.scalar.copy(out=y_late[:], in_=product(0, 1, EARLY, T, P, 0)[:])
         for t in range(1, PACK):
-            for h in range(HALVES):
-                acc = product(t, h, BANK * h, BANK, BANK, "bank%d" % (2 * t + h))
+            for h in range(T // BANK):
+                acc = product(t, h, BANK * h, BANK * (h + 1), BANK, 2 * t + h)
                 nc.scalar.copy(out=y[t][:, BANK * h : BANK * (h + 1)], in_=acc[:])
 
-        rounded = keep.tile([P, U], BF16, name="rounded")
-        rounded_first = keep.tile([P, FIRST_MOVE], BF16, name="rounded_first", tag="odd1", align_bytes=64)
+        rounded = keep.tile([P, U], BF16, name="rounded", tag="w1st_codes", align_bytes=64)
+        rounded_first = keep.tile([P, FIRST_MOVE], BF16, name="rounded_first", tag="w23_codes0", align_bytes=64)
         by_col = grouped[:].rearrange("p (c d v) -> p c d v", d=2, v=2)
 
-        def pairs_of(c0, c1):
-            base = 0 if c0 < FIRST_MOVE else FIRST_MOVE
-            return moved[base][:].rearrange("p v c -> p c v")[:, c0 - base : c1 - base, :]
-
         def scatter(t, values, j0, j1):
-            nc.vector.tensor_copy(window[t][:].indirect(offsets[:, j0 // 16 : j1 // 16]), values)
+            nc.vector.tensor_copy(window[t][:].indirect(offsets[:, j0 // LIST_ROWS : j1 // LIST_ROWS]), values)
 
-        for t in range(PACK):
-            if t == 0:
-                scatter(t, y[t][:, 0:EARLY], 0, EARLY)
-                scatter(t, y_late[:], EARLY, T)
-            elif t == 1:
-                scatter(t, y[t][:, 0:BANK], 0, BANK)
-                scatter(t, y[t][:, BANK:T], BANK, T)
-            else:
-                scatter(t, y[t][:], 0, T)
+        def store(t):
             nc.sync.dma_start(out=rows_of(out_0, t), in_=window[t][:])
-            if t < 2:
-                if t == 0:
-                    gpsimd_copy(out=rounded[:], in_=window[t][:])
-                for c0, c1 in MOVE_PIECES if t == 1 else reversed(MOVE_PIECES):
-                    staged = rounded_first[:] if t == 1 and c0 == 0 else rounded[:, c0:c1]
-                    if t == 1:
-                        nc.scalar.copy(out=staged, in_=window[t][:, c0:c1])
-                    nc.scalar.dma_start(out=moved[c0][HP * t : HP * (t + 1), :, :], in_=staged)
-            elif t == 2:
-                cj = PAIR_SPLIT - JOINT
-                for c0, c1 in ((0, FIRST_MOVE), (FIRST_MOVE, cj)):
-                    nc.scalar.copy(out=by_col[:, c0:c1, 0, :], in_=pairs_of(c0, c1))
-                joint = pairs_of(cj, PAIR_SPLIT).unsqueeze(2).to_broadcast([P, JOINT, 2, 2])
-                nc.scalar.copy(out=by_col[:, cj:PAIR_SPLIT, :, :], in_=joint)
-                for copy, c0, c1 in ((gpsimd_copy, 0, THIRD_SPLIT), (nc.scalar.copy, THIRD_SPLIT, U)):
-                    copy(out=by_col[:, c0:c1, 1, :], in_=window[t][:, c0:c1].unsqueeze(2).to_broadcast([P, c1 - c0, 2]))
-                gpsimd_copy(out=by_col[:, PAIR_SPLIT:U, 0, :], in_=pairs_of(PAIR_SPLIT, U))
 
-        last = PACK - 1
+        def move(t, c0, staged):
+            nc.scalar.dma_start(out=moved[c0][HALF_P * t : HALF_P * (t + 1), :, :], in_=staged)
+
+        scatter(0, y[0][:, 0:EARLY], 0, EARLY)
+        scatter(0, y_late[:], EARLY, T)
+        store(0)
+        gpsimd_copy(out=rounded[:], in_=window[0][:])
+        for c0, c1 in MOVE_PIECES[1:] + MOVE_PIECES[:1]:
+            move(0, c0, rounded[:, c0:c1])
+
+        scatter(1, y[1][:, 0:BANK], 0, BANK)
+        scatter(1, y[1][:, BANK:T], BANK, T)
+        store(1)
+        for c0, c1 in MOVE_PIECES:
+            staged = rounded_first[:] if c0 == 0 else rounded[:, c0:c1]
+            nc.scalar.copy(out=staged, in_=window[1][:, c0:c1])
+            move(1, c0, staged)
+
+        scatter(2, y[2][:], 0, T)
+        store(2)
+        joint_start = U - JOINT
+        for c0, c1 in MOVE_PIECES:
+            pairs = moved[c0][:].rearrange("p v c -> p c v")
+            end = min(c1, joint_start)
+            dst = by_col[:, c0:end, 0, :].rearrange("p (c i) v -> p c v i", i=RUN)
+            nc.scalar.copy(out=dst, in_=pairs[:, 0 : end - c0, :].rearrange("p (c i) v -> p c v i", i=RUN))
+        joint = pairs[:, joint_start - c0 :, :].unsqueeze(2).to_broadcast([P, JOINT, 2, 2])
+        nc.scalar.copy(out=by_col[:, joint_start:U, :, :], in_=joint)
+        for copy, c0, c1 in ((gpsimd_copy, 0, THIRD_SPLIT), (nc.scalar.copy, THIRD_SPLIT, U)):
+            copy(out=by_col[:, c0:c1, 1, :], in_=window[2][:, c0:c1].unsqueeze(2).to_broadcast([P, c1 - c0, 2]))
+
+        scatter(3, y[3][:], 0, T)
+        store(3)
         for c0, c1 in VECTOR_PIECES:
-            nc.vector.tensor_copy(out=by_col[:, c0:c1, 1, 1], in_=window[last][:, c0:c1])
+            nc.vector.tensor_copy(out=by_col[:, c0:c1, 1, 1], in_=window[3][:, c0:c1])
         for c0, c1 in SCALAR_PIECES:
-            nc.scalar.copy(out=by_col[:, c0:c1, 1, 1], in_=window[last][:, c0:c1])
+            nc.scalar.copy(out=by_col[:, c0:c1, 1, 1], in_=window[3][:, c0:c1])
         words_out = out_1[0].rearrange("p c r -> p (c r)").bitcast(I32)
         for c0, c1 in QUANT_PIECES:
             quantize(out_codes, out_scales, grouped, c0, c1)

@@ -1,6 +1,7 @@
 from contextlib import ExitStack
 
 import concourse.mybir as mybir
+from concourse.masks import make_identity
 
 K, T, N, U = 1024, 1024, 512, 2048
 FLOPS = 2 * K * T * N
@@ -25,14 +26,10 @@ HALF_P = P // 2
 EARLY = 640
 LATE = T - EARLY
 X_PIECES = ((0, EARLY), (BANK, T))
-FIRST_MOVE = 512
-MOVE_PIECES = ((0, FIRST_MOVE), (FIRST_MOVE, 1024), (1024, U))
-THIRD_SPLIT = 1776
-RUN = 4
-JOINT = 16
-VECTOR_PIECES = ((0, 512), (512, 1024))
-SCALAR_PIECES = ((1024, 1792), (1792, 2048))
-QUANT_PIECES = VECTOR_PIECES + ((1024, 1536), (1536, 1792), (1792, 2048))
+THIRD_SPLIT = 1024
+SCALAR_PIECES = ((1024, 1536), (1536, 1792), (1792, 2048))
+QUANT = 256
+STORE_PIECES = ((0, 512), (512, 1024), (1024, 1536), (1536, 1792), (1792, 2048))
 
 
 def tile_picked_wkvput_none_lo_kernel(tc, x_words, x_scales, mem, w1, slot, out_0, out_1, out_2):
@@ -66,10 +63,12 @@ def tile_picked_wkvput_none_lo_kernel(tc, x_words, x_scales, mem, w1, slot, out_
         x_sc = [keep.tile([P, PASSES, j1 - j0], U8, name="x_sc%d" % j0, align_bytes=64) for j0, j1 in X_PIECES]
         window = [keep.tile([P, U], F32, name="window%d" % t) for t in range(PACK)]
         y = [keep.tile([P, T], F32, name="y%d" % t) for t in range(PACK)]
-        moved = {c0: keep.tile([P, 2, c1 - c0], BF16, name="moved%d" % c0) for c0, c1 in MOVE_PIECES}
-        grouped = keep.tile([P, U * PACK], BF16, name="grouped", align_bytes=64)
+        ident = keep.tile([P, P], F32, name="ident")
+        make_identity(nc, ident[:])
+        turned = [keep.tile([P, 2 * BANK], BF16, name="turned%d" % b) for b in range(U // BANK)]
+        grouped = [keep.tile([P, THIRD_SPLIT * PACK], BF16, name="grouped%d" % h, align_bytes=64) for h in range(2)]
         out_codes = keep.tile([P, U], U32, name="out_codes", align_bytes=64)
-        out_scales = keep.tile([P, U], U8, name="out_scales", align_bytes=64)
+        out_scales = keep.tile([P, BANK], U8, name="out_scales", align_bytes=64)
 
         def rows_of(dram, t):
             if t < 2:
@@ -161,9 +160,9 @@ def tile_picked_wkvput_none_lo_kernel(tc, x_words, x_scales, mem, w1, slot, out_
                 acc = product(t, h, BANK * h, BANK * (h + 1), BANK, 2 * t + h)
                 nc.scalar.copy(out=y[t][:, BANK * h : BANK * (h + 1)], in_=acc[:])
 
-        rounded = keep.tile([P, U], BF16, name="rounded", tag="w1st_codes", align_bytes=64)
-        rounded_first = keep.tile([P, FIRST_MOVE], BF16, name="rounded_first", tag="w23_codes0", align_bytes=64)
-        by_col = grouped[:].rearrange("p (c d v) -> p c d v", d=2, v=2)
+        def by_col(c0, c1):
+            h, d0 = divmod(c0, THIRD_SPLIT)
+            return grouped[h][:].rearrange("p (c d v) -> p c d v", d=2, v=2)[:, d0 : d0 + c1 - c0]
 
         def scatter(t, values, j0, j1):
             nc.vector.tensor_copy(window[t][:].indirect(offsets[:, j0 // LIST_ROWS : j1 // LIST_ROWS]), values)
@@ -171,48 +170,66 @@ def tile_picked_wkvput_none_lo_kernel(tc, x_words, x_scales, mem, w1, slot, out_
         def store(t):
             nc.sync.dma_start(out=rows_of(out_0, t), in_=window[t][:])
 
-        def move(t, c0, staged):
-            nc.scalar.dma_start(out=moved[c0][HALF_P * t : HALF_P * (t + 1), :, :], in_=staged)
+        def turn(t, b):
+            acc = psum.tile([P, BANK], F32, name="turn%d_%d" % (t, b), tag="bank%d" % (4 + b))
+            for j in range(BANK // P):
+                nc.tensor.transpose(acc[:, P * j : P * (j + 1)], window[t][:, BANK * b + P * j : BANK * b + P * (j + 1)], ident[:])
+            dst = turned[b][:].rearrange("p (j s m) -> p j s m", s=2, m=P)[:, :, t, :]
+            nc.scalar.copy(out=dst, in_=acc[:].rearrange("p (j m) -> p j m", m=P))
+
+        def turn_back(b):
+            acc = psum.tile([P, BANK], F32, name="back%d" % b, tag="bank%d" % b)
+            words = turned[b][:].bitcast(F32)
+            for j in range(BANK // P):
+                nc.tensor.transpose(acc[:, P * j : P * (j + 1)], words[:, P * j : P * (j + 1)], ident[:])
+            h, d0 = divmod(BANK * b, THIRD_SPLIT)
+            dst = grouped[h][:].bitcast(F32).rearrange("p (c d) -> p c d", d=2)[:, d0 : d0 + BANK]
+            nc.scalar.copy(out=dst, in_=acc[:].unsqueeze(2).to_broadcast([P, BANK, 2]))
 
         scatter(0, y[0][:, 0:EARLY], 0, EARLY)
         scatter(0, y_late[:], EARLY, T)
         store(0)
-        gpsimd_copy(out=rounded[:], in_=window[0][:])
-        for c0, c1 in MOVE_PIECES[1:] + MOVE_PIECES[:1]:
-            move(0, c0, rounded[:, c0:c1])
+        for b in range(U // BANK):
+            turn(0, b)
 
         scatter(1, y[1][:, 0:BANK], 0, BANK)
         scatter(1, y[1][:, BANK:T], BANK, T)
         store(1)
-        for c0, c1 in MOVE_PIECES:
-            staged = rounded_first[:] if c0 == 0 else rounded[:, c0:c1]
-            nc.scalar.copy(out=staged, in_=window[1][:, c0:c1])
-            move(1, c0, staged)
+        for b in range(U // BANK):
+            turn(1, b)
+        for b in range(U // BANK):
+            turn_back(b)
 
         scatter(2, y[2][:], 0, T)
         store(2)
-        joint_start = U - JOINT
-        for c0, c1 in MOVE_PIECES:
-            pairs = moved[c0][:].rearrange("p v c -> p c v")
-            end = min(c1, joint_start)
-            dst = by_col[:, c0:end, 0, :].rearrange("p (c i) v -> p c v i", i=RUN)
-            nc.scalar.copy(out=dst, in_=pairs[:, 0 : end - c0, :].rearrange("p (c i) v -> p c v i", i=RUN))
-        joint = pairs[:, joint_start - c0 :, :].unsqueeze(2).to_broadcast([P, JOINT, 2, 2])
-        nc.scalar.copy(out=by_col[:, joint_start:U, :, :], in_=joint)
         for copy, c0, c1 in ((gpsimd_copy, 0, THIRD_SPLIT), (nc.scalar.copy, THIRD_SPLIT, U)):
-            copy(out=by_col[:, c0:c1, 1, :], in_=window[2][:, c0:c1].unsqueeze(2).to_broadcast([P, c1 - c0, 2]))
+            copy(out=by_col(c0, c1)[:, :, 1, :], in_=window[2][:, c0:c1].unsqueeze(2).to_broadcast([P, c1 - c0, 2]))
 
         scatter(3, y[3][:], 0, T)
         store(3)
-        for c0, c1 in VECTOR_PIECES:
-            nc.vector.tensor_copy(out=by_col[:, c0:c1, 1, 1], in_=window[3][:, c0:c1])
-        for c0, c1 in SCALAR_PIECES:
-            nc.scalar.copy(out=by_col[:, c0:c1, 1, 1], in_=window[3][:, c0:c1])
         words_out = out_1[0].rearrange("p c r -> p (c r)").bitcast(I32)
-        for c0, c1 in QUANT_PIECES:
-            quantize(out_codes, out_scales, grouped, c0, c1)
-            nc.sync.dma_start(out=words_out[:, c0:c1], in_=out_codes[:, c0:c1].bitcast(I32))
+
+        def round_last(copy, c0, c1):
+            copy(out=by_col(c0, c1)[:, :, 1, 1], in_=window[3][:, c0:c1])
+
+        def quantize_out(s0, s1):
+            for c0 in range(s0, s1, QUANT):
+                b, d0 = divmod(c0, BANK)
+                nc.vector.quantize_mx(
+                    out=out_codes[:, c0 : c0 + QUANT].bitcast(FP8X4),
+                    scales=out_scales[4 * b :, d0 : d0 + QUANT],
+                    in_=by_col(c0, c0 + QUANT).rearrange("p c d v -> p (c d v)"),
+                )
+            nc.sync.dma_start(out=words_out[:, s0:s1], in_=out_codes[:, s0:s1].bitcast(I32))
+
+        for c0, c1 in SCALAR_PIECES:
+            round_last(nc.scalar.copy, c0, c1)
+        round_last(nc.vector.tensor_copy, 0, 512)
+        round_last(nc.vector.tensor_copy, 512, 768)
+        quantize_out(0, 512)
+        round_last(nc.vector.tensor_copy, 768, 1024)
+        for s0, s1 in STORE_PIECES[1:]:
+            quantize_out(s0, s1)
         for q in (0, 2, 1, 3):
-            nc.sync.dma_start(
-                out=out_2[0, 4 * q : 4 * q + 4, :].bitcast(I32), in_=out_scales[32 * q : 32 * q + 4, :].bitcast(I32)
-            )
+            rows = out_2[0, 4 * q : 4 * q + 4, :].bitcast(I32).rearrange("r (j c) -> j r c", j=4)
+            nc.sync.dma_start(out=rows, in_=out_scales[32 * q : 32 * q + 16, :].bitcast(I32))

@@ -25,7 +25,8 @@ HALF_P = P // 2
 
 EARLY = 640
 LATE = T - EARLY
-X_PIECES = ((0, EARLY), (BANK, T))
+X_PIECES = ((0, EARLY), (EARLY, T))
+FIRST = 256
 THIRD_SPLIT = 1024
 SCALAR_PIECES = ((1024, 1536), (1536, 1792), (1792, 2048))
 QUANT = 256
@@ -79,22 +80,27 @@ def tile_picked_wkvput_none_lo_kernel(tc, x_words, x_scales, mem, w1, slot, out_
             rows = w1[P * PACK * g : P * PACK * (g + 1), SIDE * s : SIDE * (s + 1)]
             nc.sync.dma_start(out=w_raw[s][g][:], in_=rows.rearrange("(p j) n -> p j n", j=PACK))
 
-        def load_x(h):
+        def load_x_scales(h):
             j0, j1 = X_PIECES[h]
             for q in range(4):
                 rows = x_scales[:, 4 * q : 4 * q + 4, j0:j1].rearrange("g r n -> r g n")
                 nc.sync.dma_start(out=x_sc[h][32 * q : 32 * q + 4, :, :].bitcast(I32), in_=rows.bitcast(I32))
+
+        def load_x_words(h):
+            j0, j1 = X_PIECES[h]
             words = x_words[:, :, 2 * j0 : 2 * j1].rearrange("g p n -> p g n")
             nc.sync.dma_start(out=x_codes[h][:].bitcast(I32), in_=words.bitcast(I32))
 
         load_w(0, 0)
         load_w(0, 1)
-        load_x(0)
+        load_x_scales(0)
+        load_x_words(0)
         nc.sync.dma_start(out=window[0][:], in_=rows_of(mem, 0))
         nc.sync.dma_start(offsets[:], slot)
         load_w(1, 0)
-        load_x(1)
+        load_x_scales(1)
         load_w(1, 1)
+        load_x_words(1)
         for t in range(1, PACK):
             nc.sync.dma_start(out=window[t][:], in_=rows_of(mem, t))
 
@@ -121,10 +127,11 @@ def tile_picked_wkvput_none_lo_kernel(tc, x_words, x_scales, mem, w1, slot, out_
                 return w1st_codes[:, P * g : P * (g + 1)], w1st_scales[:, P * g : P * (g + 1)]
             return w23_codes[g][:, P * (t - 2) : P * (t - 1)], w23_scales[g][:, P * (t - 2) : P * (t - 1)]
 
-        def product(t, h, j0, j1, width, bank):
+        def product(t, j0, j1, width, bank):
             acc = psum.tile([P, j1 - j0], F32, name="acc%d_%d" % (t, j0), tag="bank%d" % bank)
             order = range(PASSES) if t < 2 else range(PASSES - 1, -1, -1)
             for c0 in range(0, j1 - j0, width):
+                h = 0 if j0 + c0 < EARLY else 1
                 x0 = j0 + c0 - X_PIECES[h][0]
                 for g in order:
                     codes, scales = weights_of(t, g)
@@ -144,20 +151,22 @@ def tile_picked_wkvput_none_lo_kernel(tc, x_words, x_scales, mem, w1, slot, out_
             deal_23(nc.vector.tensor_copy, 0, g)
             quantize(w0_codes[g], w0_scales[g], w0_bf[g], 0, P)
             quantize_23(0, g)
-        nc.scalar.copy(out=y[0][:, 0:BANK], in_=product(0, 0, 0, BANK, BANK, 0)[:])
-        nc.vector.tensor_copy(out=y[0][:, BANK:EARLY], in_=product(0, 0, BANK, EARLY, P, 1)[:])
+        nc.scalar.copy(out=y[0][:, 0:BANK], in_=product(0, 0, BANK, BANK, 0)[:])
+        nc.vector.tensor_copy(out=y[0][:, BANK:EARLY], in_=product(0, BANK, EARLY, P, 1)[:])
 
         for g in range(PASSES):
             deal_pairs(nc.scalar.copy, w1st_bf[:, PACK * P * g : PACK * P * (g + 1)], 1, g)
             deal_23(nc.scalar.copy, 1, g)
-        quantize_23(1, 0)
         quantize(w1st_codes, w1st_scales, w1st_bf, 0, PASSES * P)
-        quantize_23(1, 1)
-        y_late = keep.tile([P, LATE], F32, name="y_late", tag="w_raw1_1")
-        nc.scalar.copy(out=y_late[:], in_=product(0, 1, EARLY, T, P, 0)[:])
-        for t in range(1, PACK):
+        for g in range(PASSES):
+            quantize_23(1, g)
+        y_late = keep.tile([P, LATE], F32, name="y_late")
+        nc.scalar.copy(out=y_late[:], in_=product(0, EARLY, T, P, 0)[:])
+        for j0, j1, bank in ((0, FIRST, 1), (FIRST, FIRST + BANK, 2), (FIRST + BANK, T, 3)):
+            nc.scalar.copy(out=y[1][:, j0:j1], in_=product(1, j0, j1, P, bank)[:])
+        for t in range(2, PACK):
             for h in range(T // BANK):
-                acc = product(t, h, BANK * h, BANK * (h + 1), BANK, 2 * t + h)
+                acc = product(t, BANK * h, BANK * (h + 1), P if h else BANK, 2 * t + h)
                 nc.scalar.copy(out=y[t][:, BANK * h : BANK * (h + 1)], in_=acc[:])
 
         def by_col(c0, c1):
@@ -192,8 +201,8 @@ def tile_picked_wkvput_none_lo_kernel(tc, x_words, x_scales, mem, w1, slot, out_
         for b in range(U // BANK):
             turn(0, b)
 
-        scatter(1, y[1][:, 0:BANK], 0, BANK)
-        scatter(1, y[1][:, BANK:T], BANK, T)
+        scatter(1, y[1][:, 0:FIRST], 0, FIRST)
+        scatter(1, y[1][:, FIRST:T], FIRST, T)
         store(1)
         for b in range(U // BANK):
             turn(1, b)
@@ -232,4 +241,5 @@ def tile_picked_wkvput_none_lo_kernel(tc, x_words, x_scales, mem, w1, slot, out_
             quantize_out(s0, s1)
         for q in (0, 2, 1, 3):
             rows = out_2[0, 4 * q : 4 * q + 4, :].bitcast(I32).rearrange("r (j c) -> j r c", j=4)
-            nc.sync.dma_start(out=rows, in_=out_scales[32 * q : 32 * q + 16, :].bitcast(I32))
+            queue = nc.sync if q < 2 else nc.scalar
+            queue.dma_start(out=rows, in_=out_scales[32 * q : 32 * q + 16, :].bitcast(I32))

@@ -27,7 +27,7 @@ EARLY = 640
 LATE = T - EARLY
 X_PIECES = ((0, EARLY), (EARLY, T))
 FIRST = 256
-THIRD_SPLIT = 1024
+GROUPS = ((0, 1024), (1024, 1792), (1792, 2048))
 SCALAR_PIECES = ((1024, 1536), (1536, 1792), (1792, 2048))
 QUANT = 256
 STORE_PIECES = ((0, 512), (512, 1024), (1024, 1536), (1536, 1792), (1792, 2048))
@@ -60,14 +60,14 @@ def tile_picked_wkvput_none_lo_kernel(tc, x_words, x_scales, mem, w1, slot, out_
             keep.tile([P, 2 * P], U32, name="w23_codes%d" % g, tag="w23_codes%d" % g, align_bytes=64) for g in range(PASSES)
         ]
         w23_scales = [keep.tile([P, 2 * P], U8, name="w23_scales%d" % g, align_bytes=64) for g in range(PASSES)]
-        x_codes = [keep.tile([P, PASSES, 2 * (j1 - j0)], U8, name="x_codes%d" % j0, align_bytes=64) for j0, j1 in X_PIECES]
+        x_codes = [keep.tile([P, PASSES, 2 * (j1 - j0)], U8, name="x_codes%d" % j0, tag="x_codes%d" % j0, align_bytes=64) for j0, j1 in X_PIECES]
         x_sc = [keep.tile([P, PASSES, j1 - j0], U8, name="x_sc%d" % j0, align_bytes=64) for j0, j1 in X_PIECES]
-        window = [keep.tile([P, U], F32, name="window%d" % t) for t in range(PACK)]
+        window = [keep.tile([P, U], F32, name="window%d" % t) for t in range(PACK - 1)]
         y = [keep.tile([P, T], F32, name="y%d" % t) for t in range(PACK)]
         ident = keep.tile([P, P], F32, name="ident")
         make_identity(nc, ident[:])
         turned = [keep.tile([P, 2 * BANK], BF16, name="turned%d" % b) for b in range(U // BANK)]
-        grouped = [keep.tile([P, THIRD_SPLIT * PACK], BF16, name="grouped%d" % h, align_bytes=64) for h in range(2)]
+        grouped = {c0: keep.tile([P, (c1 - c0) * PACK], BF16, name="grouped%d" % c0, align_bytes=64) for c0, c1 in GROUPS}
         out_codes = keep.tile([P, U], U32, name="out_codes", align_bytes=64)
         out_scales = keep.tile([P, BANK], U8, name="out_scales", align_bytes=64)
 
@@ -101,7 +101,7 @@ def tile_picked_wkvput_none_lo_kernel(tc, x_words, x_scales, mem, w1, slot, out_
         load_x_scales(1)
         load_w(1, 1)
         load_x_words(1)
-        for t in range(1, PACK):
+        for t in (2, 1):
             nc.sync.dma_start(out=window[t][:], in_=rows_of(mem, t))
 
         def deal_pairs(copy, dst, s, g):
@@ -162,16 +162,16 @@ def tile_picked_wkvput_none_lo_kernel(tc, x_words, x_scales, mem, w1, slot, out_
             quantize_23(1, g)
         y_late = keep.tile([P, LATE], F32, name="y_late")
         nc.scalar.copy(out=y_late[:], in_=product(0, EARLY, T, P, 0)[:])
-        for j0, j1, bank in ((0, FIRST, 1), (FIRST, FIRST + BANK, 2), (FIRST + BANK, T, 3)):
-            nc.scalar.copy(out=y[1][:, j0:j1], in_=product(1, j0, j1, P, bank)[:])
-        for t in range(2, PACK):
-            for h in range(T // BANK):
-                acc = product(t, BANK * h, BANK * (h + 1), P if h else BANK, 2 * t + h)
-                nc.scalar.copy(out=y[t][:, BANK * h : BANK * (h + 1)], in_=acc[:])
+        nc.scalar.copy(out=y[2][:, 0:FIRST], in_=product(2, 0, FIRST, P, 1)[:])
+        for t, j0, j1, width, bank in (
+            (1, 0, BANK, BANK, 2),
+            (1, BANK, T, P, 3),
+        ):
+            nc.scalar.copy(out=y[t][:, j0:j1], in_=product(t, j0, j1, width, bank)[:])
 
         def by_col(c0, c1):
-            h, d0 = divmod(c0, THIRD_SPLIT)
-            return grouped[h][:].rearrange("p (c d v) -> p c d v", d=2, v=2)[:, d0 : d0 + c1 - c0]
+            g0 = max(g for g in grouped if g <= c0)
+            return grouped[g0][:].rearrange("p (c d v) -> p c d v", d=2, v=2)[:, c0 - g0 : c1 - g0]
 
         def scatter(t, values, j0, j1):
             nc.vector.tensor_copy(window[t][:].indirect(offsets[:, j0 // LIST_ROWS : j1 // LIST_ROWS]), values)
@@ -180,38 +180,47 @@ def tile_picked_wkvput_none_lo_kernel(tc, x_words, x_scales, mem, w1, slot, out_
             nc.sync.dma_start(out=rows_of(out_0, t), in_=window[t][:])
 
         def turn(t, b):
-            acc = psum.tile([P, BANK], F32, name="turn%d_%d" % (t, b), tag="bank%d" % (4 + b))
+            acc = psum.tile([P, BANK], F32, name="turn%d_%d" % (t, b), tag="bank%d" % ((b + 2) % 4))
             for j in range(BANK // P):
                 nc.tensor.transpose(acc[:, P * j : P * (j + 1)], window[t][:, BANK * b + P * j : BANK * b + P * (j + 1)], ident[:])
             dst = turned[b][:].rearrange("p (j s m) -> p j s m", s=2, m=P)[:, :, t, :]
             nc.scalar.copy(out=dst, in_=acc[:].rearrange("p (j m) -> p j m", m=P))
 
         def turn_back(b):
-            acc = psum.tile([P, BANK], F32, name="back%d" % b, tag="bank%d" % b)
+            acc = psum.tile([P, BANK], F32, name="back%d" % b, tag="bank%d" % (4 + b))
             words = turned[b][:].bitcast(F32)
             for j in range(BANK // P):
                 nc.tensor.transpose(acc[:, P * j : P * (j + 1)], words[:, P * j : P * (j + 1)], ident[:])
-            h, d0 = divmod(BANK * b, THIRD_SPLIT)
-            dst = grouped[h][:].bitcast(F32).rearrange("p (c d) -> p c d", d=2)[:, d0 : d0 + BANK]
-            nc.scalar.copy(out=dst, in_=acc[:].unsqueeze(2).to_broadcast([P, BANK, 2]))
+            for g0, g1 in GROUPS:
+                c0, c1 = max(g0, BANK * b), min(g1, BANK * (b + 1))
+                if c0 < c1:
+                    dst = grouped[g0][:].bitcast(F32).rearrange("p (c d) -> p c d", d=2)[:, c0 - g0 : c1 - g0]
+                    src = acc[:, c0 - BANK * b : c1 - BANK * b].unsqueeze(2).to_broadcast([P, c1 - c0, 2])
+                    nc.scalar.copy(out=dst, in_=src)
 
+        for j0, j1, width, bank in ((0, BANK, BANK, 0), (BANK, T, P, 1)):
+            nc.scalar.copy(out=y[3][:, j0:j1], in_=product(3, j0, j1, width, bank)[:])
         scatter(0, y[0][:, 0:EARLY], 0, EARLY)
         scatter(0, y_late[:], EARLY, T)
         store(0)
         for b in range(U // BANK):
             turn(0, b)
+        for j0, j1, bank in ((256, 512, 2), (512, 768, 3), (768, 896, 0), (896, 1024, 1)):
+            nc.scalar.copy(out=y[2][:, j0:j1], in_=product(2, j0, j1, P, bank)[:])
+        window.append(keep.tile([P, U], F32, name="window3", tag="x_codes%d" % EARLY, align_bytes=64))
+        nc.scalar.dma_start(out=window[3][:], in_=rows_of(mem, 3))
 
-        scatter(1, y[1][:, 0:FIRST], 0, FIRST)
-        scatter(1, y[1][:, FIRST:T], FIRST, T)
+        scatter(2, y[2][:, 0:FIRST], 0, FIRST)
+        scatter(1, y[1][:], 0, T)
         store(1)
         for b in range(U // BANK):
             turn(1, b)
         for b in range(U // BANK):
             turn_back(b)
 
-        scatter(2, y[2][:], 0, T)
+        scatter(2, y[2][:, FIRST:T], FIRST, T)
         store(2)
-        for copy, c0, c1 in ((gpsimd_copy, 0, THIRD_SPLIT), (nc.scalar.copy, THIRD_SPLIT, U)):
+        for copy, (c0, c1) in zip((gpsimd_copy, nc.scalar.copy, gpsimd_copy), GROUPS):
             copy(out=by_col(c0, c1)[:, :, 1, :], in_=window[2][:, c0:c1].unsqueeze(2).to_broadcast([P, c1 - c0, 2]))
 
         scatter(3, y[3][:], 0, T)

@@ -27,7 +27,8 @@ EARLY = 640
 LATE = T - EARLY
 X_PIECES = ((0, EARLY), (EARLY, T))
 FIRST = 256
-GROUPS = ((0, 1024), (1024, 1792), (1792, 2048))
+GROUPS = ((0, 1024), (1024, 1536), (1536, 2048))
+TURN_ORDER = (0, 1, 2, 3)
 SCALAR_PIECES = ((1024, 1536), (1536, 1792), (1792, 2048))
 QUANT = 256
 STORE_PIECES = ((0, 512), (512, 1024), (1024, 1536), (1536, 1792), (1792, 2048))
@@ -180,7 +181,7 @@ def tile_picked_wkvput_none_lo_kernel(tc, x_words, x_scales, mem, w1, slot, out_
             nc.sync.dma_start(out=rows_of(out_0, t), in_=window[t][:])
 
         def turn(t, b):
-            acc = psum.tile([P, BANK], F32, name="turn%d_%d" % (t, b), tag="bank%d" % ((b + 2) % 4))
+            acc = psum.tile([P, BANK], F32, name="turn%d_%d" % (t, b), tag="bank%d" % ((TURN_ORDER.index(b) + 2) % 4))
             for j in range(BANK // P):
                 nc.tensor.transpose(acc[:, P * j : P * (j + 1)], window[t][:, BANK * b + P * j : BANK * b + P * (j + 1)], ident[:])
             dst = turned[b][:].rearrange("p (j s m) -> p j s m", s=2, m=P)[:, :, t, :]
@@ -191,19 +192,20 @@ def tile_picked_wkvput_none_lo_kernel(tc, x_words, x_scales, mem, w1, slot, out_
             words = turned[b][:].bitcast(F32)
             for j in range(BANK // P):
                 nc.tensor.transpose(acc[:, P * j : P * (j + 1)], words[:, P * j : P * (j + 1)], ident[:])
-            for g0, g1 in GROUPS:
-                c0, c1 = max(g0, BANK * b), min(g1, BANK * (b + 1))
-                if c0 < c1:
-                    dst = grouped[g0][:].bitcast(F32).rearrange("p (c d) -> p c d", d=2)[:, c0 - g0 : c1 - g0]
-                    src = acc[:, c0 - BANK * b : c1 - BANK * b].unsqueeze(2).to_broadcast([P, c1 - c0, 2])
-                    nc.scalar.copy(out=dst, in_=src)
+            c0, c1 = BANK * b, BANK * (b + 1)
+            if c0 == GROUPS[2][0]:
+                nc.scalar.copy(out=by_col(c0, c1)[:, :, 0, :], in_=acc[:].bitcast(BF16).rearrange("p (c v) -> p c v", v=2))
+            else:
+                g0 = max(g for g in grouped if g <= c0)
+                dst = grouped[g0][:].bitcast(F32).rearrange("p (c d) -> p c d", d=2)[:, c0 - g0 : c1 - g0]
+                nc.scalar.copy(out=dst, in_=acc[:].unsqueeze(2).to_broadcast([P, BANK, 2]))
 
         for j0, j1, width, bank in ((0, BANK, BANK, 0), (BANK, T, P, 1)):
             nc.scalar.copy(out=y[3][:, j0:j1], in_=product(3, j0, j1, width, bank)[:])
         scatter(0, y[0][:, 0:EARLY], 0, EARLY)
         scatter(0, y_late[:], EARLY, T)
         store(0)
-        for b in range(U // BANK):
+        for b in TURN_ORDER:
             turn(0, b)
         for j0, j1, bank in ((256, 512, 2), (512, 768, 3), (768, 896, 0), (896, 1024, 1)):
             nc.scalar.copy(out=y[2][:, j0:j1], in_=product(2, j0, j1, P, bank)[:])
@@ -213,14 +215,14 @@ def tile_picked_wkvput_none_lo_kernel(tc, x_words, x_scales, mem, w1, slot, out_
         scatter(2, y[2][:, 0:FIRST], 0, FIRST)
         scatter(1, y[1][:], 0, T)
         store(1)
-        for b in range(U // BANK):
+        for b in TURN_ORDER:
             turn(1, b)
-        for b in range(U // BANK):
+        for b in TURN_ORDER:
             turn_back(b)
 
         scatter(2, y[2][:, FIRST:T], FIRST, T)
         store(2)
-        for copy, (c0, c1) in zip((gpsimd_copy, nc.scalar.copy, gpsimd_copy), GROUPS):
+        for copy, (c0, c1) in ((gpsimd_copy, GROUPS[2]), (gpsimd_copy, GROUPS[0]), (nc.scalar.copy, GROUPS[1])):
             copy(out=by_col(c0, c1)[:, :, 1, :], in_=window[2][:, c0:c1].unsqueeze(2).to_broadcast([P, c1 - c0, 2]))
 
         scatter(3, y[3][:], 0, T)

@@ -156,17 +156,19 @@ def tile_picked_wkvput_none_lo_kernel(tc, x_words, x_scales, mem, w1, slot, out_
         nc.vector.tensor_copy(out=y[0][:, BANK:EARLY], in_=product(0, BANK, EARLY, P, 1)[:])
 
         for g in range(PASSES):
-            deal_pairs(nc.scalar.copy, w1st_bf[:, PACK * P * g : PACK * P * (g + 1)], 1, g)
             deal_23(nc.scalar.copy, 1, g)
-        quantize(w1st_codes, w1st_scales, w1st_bf, 0, PASSES * P)
+            deal_pairs(nc.scalar.copy, w1st_bf[:, PACK * P * g : PACK * P * (g + 1)], 1, g)
         for g in range(PASSES):
             quantize_23(1, g)
+        quantize(w1st_codes, w1st_scales, w1st_bf, 0, PASSES * P)
         y_late = keep.tile([P, LATE], F32, name="y_late")
         nc.scalar.copy(out=y_late[:], in_=product(0, EARLY, T, P, 0)[:])
         nc.scalar.copy(out=y[2][:, 0:FIRST], in_=product(2, 0, FIRST, P, 1)[:])
         for t, j0, j1, width, bank in (
-            (1, 0, BANK, BANK, 2),
-            (1, BANK, T, P, 3),
+            (1, 0, 512, BANK, 2),
+            (1, 512, 768, P, 3),
+            (1, 768, 896, P, 0),
+            (1, 896, 1024, P, 1),
         ):
             nc.scalar.copy(out=y[t][:, j0:j1], in_=product(t, j0, j1, width, bank)[:])
 
@@ -181,7 +183,7 @@ def tile_picked_wkvput_none_lo_kernel(tc, x_words, x_scales, mem, w1, slot, out_
             nc.sync.dma_start(out=rows_of(out_0, t), in_=window[t][:])
 
         def turn(t, b):
-            acc = psum.tile([P, BANK], F32, name="turn%d_%d" % (t, b), tag="bank%d" % ((TURN_ORDER.index(b) + 2) % 4))
+            acc = psum.tile([P, BANK], F32, name="turn%d_%d" % (t, b), tag="bank%d" % b)
             for j in range(BANK // P):
                 nc.tensor.transpose(acc[:, P * j : P * (j + 1)], window[t][:, BANK * b + P * j : BANK * b + P * (j + 1)], ident[:])
             dst = turned[b][:].rearrange("p (j s m) -> p j s m", s=2, m=P)[:, :, t, :]
@@ -200,17 +202,17 @@ def tile_picked_wkvput_none_lo_kernel(tc, x_words, x_scales, mem, w1, slot, out_
                 dst = grouped[g0][:].bitcast(F32).rearrange("p (c d) -> p c d", d=2)[:, c0 - g0 : c1 - g0]
                 nc.scalar.copy(out=dst, in_=acc[:].unsqueeze(2).to_broadcast([P, BANK, 2]))
 
-        for j0, j1, width, bank in ((0, BANK, BANK, 0), (BANK, T, P, 1)):
+        for j0, j1, width, bank in ((0, BANK, BANK, 2), (BANK, T, P, 3)):
             nc.scalar.copy(out=y[3][:, j0:j1], in_=product(3, j0, j1, width, bank)[:])
+        for j0, j1, bank in ((FIRST, BANK, 2), (BANK, T, 3)):
+            nc.scalar.copy(out=y[2][:, j0:j1], in_=product(2, j0, j1, P, bank)[:])
+        window.append(keep.tile([P, U], F32, name="window3", tag="x_codes%d" % EARLY, align_bytes=64))
+        nc.scalar.dma_start(out=window[3][:], in_=rows_of(mem, 3))
         scatter(0, y[0][:, 0:EARLY], 0, EARLY)
         scatter(0, y_late[:], EARLY, T)
         store(0)
         for b in TURN_ORDER:
             turn(0, b)
-        for j0, j1, bank in ((256, 512, 2), (512, 768, 3), (768, 896, 0), (896, 1024, 1)):
-            nc.scalar.copy(out=y[2][:, j0:j1], in_=product(2, j0, j1, P, bank)[:])
-        window.append(keep.tile([P, U], F32, name="window3", tag="x_codes%d" % EARLY, align_bytes=64))
-        nc.scalar.dma_start(out=window[3][:], in_=rows_of(mem, 3))
 
         scatter(2, y[2][:, 0:FIRST], 0, FIRST)
         scatter(1, y[1][:], 0, T)

@@ -27,8 +27,8 @@ EARLY = 640
 LATE = T - EARLY
 X_PIECES = ((0, EARLY), (EARLY, T))
 FIRST = 256
-GROUPS = ((0, 1024), (1024, 1536), (1536, 2048))
-TURN_ORDER = (0, 1, 2, 3)
+GROUPS = ((0, 512), (512, 1536), (1536, 2048))
+TURN_ORDER = (1, 2, 3, 0)
 SCALAR_PIECES = ((1024, 1536), (1536, 1792), (1792, 2048))
 QUANT = 256
 STORE_PIECES = ((0, 512), (512, 1024), (1024, 1536), (1536, 1792), (1792, 2048))
@@ -61,13 +61,12 @@ def tile_picked_wkvput_none_lo_kernel(tc, x_words, x_scales, mem, w1, slot, out_
             keep.tile([P, 2 * P], U32, name="w23_codes%d" % g, tag="w23_codes%d" % g, align_bytes=64) for g in range(PASSES)
         ]
         w23_scales = [keep.tile([P, 2 * P], U8, name="w23_scales%d" % g, align_bytes=64) for g in range(PASSES)]
-        x_codes = [keep.tile([P, PASSES, 2 * (j1 - j0)], U8, name="x_codes%d" % j0, tag="x_codes%d" % j0, align_bytes=64) for j0, j1 in X_PIECES]
+        x_codes = [keep.tile([P, PASSES, 2 * (j1 - j0)], U8, name="x_codes%d" % j0, align_bytes=64) for j0, j1 in X_PIECES]
         x_sc = [keep.tile([P, PASSES, j1 - j0], U8, name="x_sc%d" % j0, align_bytes=64) for j0, j1 in X_PIECES]
-        window = [keep.tile([P, U], F32, name="window%d" % t) for t in range(PACK - 1)]
+        window = [keep.tile([P, U], F32, name="window%d" % t) for t in range(PACK)]
         y = [keep.tile([P, T], F32, name="y%d" % t) for t in range(PACK)]
         ident = keep.tile([P, P], F32, name="ident")
         make_identity(nc, ident[:])
-        turned = [keep.tile([P, 2 * BANK], BF16, name="turned%d" % b) for b in range(U // BANK)]
         grouped = {c0: keep.tile([P, (c1 - c0) * PACK], BF16, name="grouped%d" % c0, align_bytes=64) for c0, c1 in GROUPS}
         out_codes = keep.tile([P, U], U32, name="out_codes", align_bytes=64)
         out_scales = keep.tile([P, BANK], U8, name="out_scales", align_bytes=64)
@@ -102,7 +101,7 @@ def tile_picked_wkvput_none_lo_kernel(tc, x_words, x_scales, mem, w1, slot, out_
         load_x_scales(1)
         load_w(1, 1)
         load_x_words(1)
-        for t in (2, 1):
+        for t in (2, 1, 3):
             nc.sync.dma_start(out=window[t][:], in_=rows_of(mem, t))
 
         def deal_pairs(copy, dst, s, g):
@@ -163,7 +162,8 @@ def tile_picked_wkvput_none_lo_kernel(tc, x_words, x_scales, mem, w1, slot, out_
         quantize(w1st_codes, w1st_scales, w1st_bf, 0, PASSES * P)
         y_late = keep.tile([P, LATE], F32, name="y_late")
         nc.scalar.copy(out=y_late[:], in_=product(0, EARLY, T, P, 0)[:])
-        nc.scalar.copy(out=y[2][:, 0:FIRST], in_=product(2, 0, FIRST, P, 1)[:])
+        y_first = keep.tile([P, FIRST], F32, name="y_first", tag="turned1")
+        nc.scalar.copy(out=y_first[:], in_=product(2, 0, FIRST, P, 1)[:])
         for t, j0, j1, width, bank in (
             (1, 0, 512, BANK, 2),
             (1, 512, 768, P, 3),
@@ -183,7 +183,7 @@ def tile_picked_wkvput_none_lo_kernel(tc, x_words, x_scales, mem, w1, slot, out_
             nc.sync.dma_start(out=rows_of(out_0, t), in_=window[t][:])
 
         def turn(t, b):
-            acc = psum.tile([P, BANK], F32, name="turn%d_%d" % (t, b), tag="bank%d" % b)
+            acc = psum.tile([P, BANK], F32, name="turn%d_%d" % (t, b), tag="bank%d" % TURN_ORDER.index(b))
             for j in range(BANK // P):
                 nc.tensor.transpose(acc[:, P * j : P * (j + 1)], window[t][:, BANK * b + P * j : BANK * b + P * (j + 1)], ident[:])
             dst = turned[b][:].rearrange("p (j s m) -> p j s m", s=2, m=P)[:, :, t, :]
@@ -195,26 +195,32 @@ def tile_picked_wkvput_none_lo_kernel(tc, x_words, x_scales, mem, w1, slot, out_
             for j in range(BANK // P):
                 nc.tensor.transpose(acc[:, P * j : P * (j + 1)], words[:, P * j : P * (j + 1)], ident[:])
             c0, c1 = BANK * b, BANK * (b + 1)
-            if c0 == GROUPS[2][0]:
+            if c0 == GROUPS[0][0]:
                 nc.scalar.copy(out=by_col(c0, c1)[:, :, 0, :], in_=acc[:].bitcast(BF16).rearrange("p (c v) -> p c v", v=2))
             else:
                 g0 = max(g for g in grouped if g <= c0)
                 dst = grouped[g0][:].bitcast(F32).rearrange("p (c d) -> p c d", d=2)[:, c0 - g0 : c1 - g0]
                 nc.scalar.copy(out=dst, in_=acc[:].unsqueeze(2).to_broadcast([P, BANK, 2]))
 
-        for j0, j1, width, bank in ((0, BANK, BANK, 2), (BANK, T, P, 3)):
-            nc.scalar.copy(out=y[3][:, j0:j1], in_=product(3, j0, j1, width, bank)[:])
-        for j0, j1, bank in ((FIRST, BANK, 2), (BANK, T, 3)):
-            nc.scalar.copy(out=y[2][:, j0:j1], in_=product(2, j0, j1, P, bank)[:])
-        window.append(keep.tile([P, U], F32, name="window3", tag="x_codes%d" % EARLY, align_bytes=64))
-        nc.scalar.dma_start(out=window[3][:], in_=rows_of(mem, 3))
         scatter(0, y[0][:, 0:EARLY], 0, EARLY)
         scatter(0, y_late[:], EARLY, T)
         store(0)
+        scatter(2, y_first[:], 0, FIRST)
+        turned = [keep.tile([P, 2 * BANK], BF16, name="turned%d" % b, tag="turned%d" % b) for b in range(U // BANK)]
         for b in TURN_ORDER:
             turn(0, b)
+        for t, j0, j1, width, bank in (
+            (2, 256, 512, P, 0),
+            (2, 512, 768, P, 1),
+            (2, 768, 896, P, 2),
+            (2, 896, 1024, P, 3),
+            (3, 0, 512, BANK, 0),
+            (3, 512, 768, P, 1),
+            (3, 768, 896, P, 2),
+            (3, 896, 1024, P, 3),
+        ):
+            nc.scalar.copy(out=y[t][:, j0:j1], in_=product(t, j0, j1, width, bank)[:])
 
-        scatter(2, y[2][:, 0:FIRST], 0, FIRST)
         scatter(1, y[1][:], 0, T)
         store(1)
         for b in TURN_ORDER:
@@ -224,7 +230,7 @@ def tile_picked_wkvput_none_lo_kernel(tc, x_words, x_scales, mem, w1, slot, out_
 
         scatter(2, y[2][:, FIRST:T], FIRST, T)
         store(2)
-        for copy, (c0, c1) in ((gpsimd_copy, GROUPS[2]), (gpsimd_copy, GROUPS[0]), (nc.scalar.copy, GROUPS[1])):
+        for copy, (c0, c1) in zip((gpsimd_copy, gpsimd_copy, nc.scalar.copy), GROUPS):
             copy(out=by_col(c0, c1)[:, :, 1, :], in_=window[2][:, c0:c1].unsqueeze(2).to_broadcast([P, c1 - c0, 2]))
 
         scatter(3, y[3][:], 0, T)
@@ -246,11 +252,9 @@ def tile_picked_wkvput_none_lo_kernel(tc, x_words, x_scales, mem, w1, slot, out_
 
         for c0, c1 in SCALAR_PIECES:
             round_last(nc.scalar.copy, c0, c1)
-        round_last(nc.vector.tensor_copy, 0, 512)
-        round_last(nc.vector.tensor_copy, 512, 768)
-        quantize_out(0, 512)
-        round_last(nc.vector.tensor_copy, 768, 1024)
-        for s0, s1 in STORE_PIECES[1:]:
+        for c0 in range(0, 1024, QUANT):
+            round_last(nc.vector.tensor_copy, c0, c0 + QUANT)
+        for s0, s1 in STORE_PIECES:
             quantize_out(s0, s1)
         for q in (0, 2, 1, 3):
             rows = out_2[0, 4 * q : 4 * q + 4, :].bitcast(I32).rearrange("r (j c) -> j r c", j=4)

@@ -1,7 +1,6 @@
 from contextlib import ExitStack
 
 import concourse.mybir as mybir
-from concourse.masks import make_identity
 
 K, T, N, U = 1024, 1024, 512, 2048
 FLOPS = 2 * K * T * N
@@ -14,22 +13,15 @@ U16 = mybir.dt.uint16
 U8 = mybir.dt.uint8
 FP8X4 = mybir.dt.float8_e4m3fn_x4
 FP4X4 = mybir.dt.float4_e2m1fn_x4
+COPY = mybir.ActivationFunctionType.Copy
 
 P = 128
 PACK = 4
 PASSES = K // (P * PACK)
 BANK = 512
 LIST_ROWS = 16
-SIDE = N // 2
-HALF_P = P // 2
-
-EARLY = 640
-LATE = T - EARLY
-X_PIECES = ((0, EARLY), (EARLY, T))
-FIRST = 256
-GROUPS = ((0, 512), (512, 1536), (1536, 2048))
-TURN_ORDER = (1, 2, 3, 0)
-SCALAR_PIECES = ((1024, 1536), (1536, 1792), (1792, 2048))
+SCALAR_SCATTERS = ((0, 384), (384, 768), (768, 1024))
+SPLIT = 1024
 QUANT = 256
 STORE_PIECES = ((0, 512), (512, 1024), (1024, 1536), (1536, 1792), (1792, 2048))
 
@@ -46,199 +38,114 @@ def tile_picked_wkvput_none_lo_kernel(tc, x_words, x_scales, mem, w1, slot, out_
             )
 
         offsets = keep.tile([P, T // LIST_ROWS], U16, name="offsets")
-        w_raw = [
-            [keep.tile([P, PACK, SIDE], F32, name="w_raw%d_%d" % (s, g), tag="w_raw%d_%d" % (s, g)) for g in range(PASSES)]
-            for s in range(2)
-        ]
-        w0_bf = [keep.tile([P, PACK * P], BF16, name="w0_bf%d" % g, align_bytes=64) for g in range(PASSES)]
-        w0_codes = [keep.tile([P, P], U32, name="w0_codes%d" % g, align_bytes=64) for g in range(PASSES)]
-        w0_scales = [keep.tile([P, P], U8, name="w0_scales%d" % g, align_bytes=64) for g in range(PASSES)]
-        w1st_bf = keep.tile([P, PASSES * PACK * P], BF16, name="w1st_bf", align_bytes=64)
-        w1st_codes = keep.tile([P, PASSES * P], U32, name="w1st_codes", tag="w1st_codes", align_bytes=64)
-        w1st_scales = keep.tile([P, PASSES * P], U8, name="w1st_scales", align_bytes=64)
-        w23_bf = [keep.tile([P, 2 * PACK * P], BF16, name="w23_bf%d" % g, align_bytes=64) for g in range(PASSES)]
-        w23_codes = [
-            keep.tile([P, 2 * P], U32, name="w23_codes%d" % g, tag="w23_codes%d" % g, align_bytes=64) for g in range(PASSES)
-        ]
-        w23_scales = [keep.tile([P, 2 * P], U8, name="w23_scales%d" % g, align_bytes=64) for g in range(PASSES)]
-        x_codes = [keep.tile([P, PASSES, 2 * (j1 - j0)], U8, name="x_codes%d" % j0, align_bytes=64) for j0, j1 in X_PIECES]
-        x_sc = [keep.tile([P, PASSES, j1 - j0], U8, name="x_sc%d" % j0, align_bytes=64) for j0, j1 in X_PIECES]
+        w_raw = [keep.tile([P, PACK, N], F32, name="w_raw%d" % g) for g in range(PASSES)]
+        w_bf = [[keep.tile([P, 2 * PACK * P], BF16, name="w_bf%d_%d" % (d, g), align_bytes=64) for g in range(PASSES)] for d in range(2)]
+        w_codes = [[keep.tile([P, 2 * P], U32, name="w_codes%d_%d" % (d, g), align_bytes=64) for g in range(PASSES)] for d in range(2)]
+        w_scales = [[keep.tile([P, 2 * P], U8, name="w_scales%d_%d" % (d, g), align_bytes=64) for g in range(PASSES)] for d in range(2)]
+        x_codes = [keep.tile([P, 2 * T], U8, name="x_codes%d" % g, align_bytes=64) for g in range(PASSES)]
+        x_sc = keep.tile([P, PASSES, T], U8, name="x_sc", align_bytes=64)
         window = [keep.tile([P, U], F32, name="window%d" % t) for t in range(PACK)]
         y = [keep.tile([P, T], F32, name="y%d" % t) for t in range(PACK)]
-        ident = keep.tile([P, P], F32, name="ident")
-        make_identity(nc, ident[:])
-        grouped = {c0: keep.tile([P, (c1 - c0) * PACK], BF16, name="grouped%d" % c0, align_bytes=64) for c0, c1 in GROUPS}
+        halves = ((0, SPLIT), (SPLIT, U))
+        pairs = [keep.tile([P, PACK * (c1 - c0)], BF16, name="pairs%d" % c0) for c0, c1 in halves]
+        grouped = [keep.tile([P, PACK * (c1 - c0)], BF16, name="grouped%d" % c0, align_bytes=64) for c0, c1 in halves]
         out_codes = keep.tile([P, U], U32, name="out_codes", align_bytes=64)
         out_scales = keep.tile([P, BANK], U8, name="out_scales", align_bytes=64)
 
         def rows_of(dram, t):
-            if t < 2:
-                return dram[SIDE * t : SIDE * (t + 1), :].rearrange("(l r) c -> l r c", r=PACK)[:, 0:2, :]
             return dram.rearrange("(p r) c -> p r c", r=PACK)[:, t, :]
 
-        def load_w(s, g):
-            rows = w1[P * PACK * g : P * PACK * (g + 1), SIDE * s : SIDE * (s + 1)]
-            nc.sync.dma_start(out=w_raw[s][g][:], in_=rows.rearrange("(p j) n -> p j n", j=PACK))
+        def load_w(g):
+            rows = w1[P * PACK * g : P * PACK * (g + 1), :]
+            nc.sync.dma_start(out=w_raw[g][:], in_=rows.rearrange("(p j) n -> p j n", j=PACK))
 
-        def load_x_scales(h):
-            j0, j1 = X_PIECES[h]
-            for q in range(4):
-                rows = x_scales[:, 4 * q : 4 * q + 4, j0:j1].rearrange("g r n -> r g n")
-                nc.sync.dma_start(out=x_sc[h][32 * q : 32 * q + 4, :, :].bitcast(I32), in_=rows.bitcast(I32))
+        def load_x_words(g):
+            nc.sync.dma_start(out=x_codes[g][:].bitcast(I32), in_=x_words[g].bitcast(I32))
 
-        def load_x_words(h):
-            j0, j1 = X_PIECES[h]
-            words = x_words[:, :, 2 * j0 : 2 * j1].rearrange("g p n -> p g n")
-            nc.sync.dma_start(out=x_codes[h][:].bitcast(I32), in_=words.bitcast(I32))
-
-        load_w(0, 0)
-        load_w(0, 1)
-        load_x_scales(0)
+        load_w(0)
+        for q in (0, 2, 1, 3):
+            rows = x_scales[:, 4 * q : 4 * q + 4, :].rearrange("g r n -> r g n")
+            nc.sync.dma_start(out=x_sc[32 * q : 32 * q + 4, :, :].bitcast(I32), in_=rows.bitcast(I32))
         load_x_words(0)
+        load_w(1)
+        load_x_words(1)
         nc.sync.dma_start(out=window[0][:], in_=rows_of(mem, 0))
         nc.sync.dma_start(offsets[:], slot)
-        load_w(1, 0)
-        load_x_scales(1)
-        load_w(1, 1)
-        load_x_words(1)
-        for t in (2, 1, 3):
+        for t in range(1, PACK):
             nc.sync.dma_start(out=window[t][:], in_=rows_of(mem, t))
 
-        def deal_pairs(copy, dst, s, g):
-            src = w_raw[s][g][:].rearrange("p j (l r) -> p l j r", r=PACK)[:, :, :, 0:2]
-            copy(out=dst.rearrange("p (l v j) -> p l j v", v=2, j=PACK), in_=src)
-
-        def deal_23(copy, s, g):
-            dst = w23_bf[g][:].rearrange("p (u s l j) -> p s l j u", u=2, s=2, j=PACK)[:, s]
-            src = w_raw[s][g][:].rearrange("p j (l r) -> p l j r", r=PACK)[:, :, :, 2:4]
+        def deal(copy, d, g):
+            dst = w_bf[d][g][:].rearrange("p (u m j) -> p m j u", u=2, j=PACK)
+            src = w_raw[g][:].rearrange("p j (m r) -> p m j r", r=PACK)[:, :, :, 2 * d : 2 * d + 2]
             copy(out=dst, in_=src)
 
-        def quantize(codes, scales, values, c0, c1):
-            nc.vector.quantize_mx(out=codes[:, c0:c1].bitcast(FP8X4), scales=scales[:, c0:c1], in_=values[:, PACK * c0 : PACK * c1])
+        def quantize_w(d, g):
+            nc.vector.quantize_mx(out=w_codes[d][g][:].bitcast(FP8X4), scales=w_scales[d][g][:], in_=w_bf[d][g][:])
 
-        def quantize_23(s, g):
-            for u in range(2):
-                quantize(w23_codes[g], w23_scales[g], w23_bf[g], P * u + HALF_P * s, P * u + HALF_P * (s + 1))
+        for g in range(PASSES):
+            deal(nc.vector.tensor_copy, 0, g)
+            deal(nc.scalar.copy, 1, g)
+            quantize_w(0, g)
+            quantize_w(1, g)
 
-        def weights_of(t, g):
-            if t == 0:
-                return w0_codes[g][:], w0_scales[g][:]
-            if t == 1:
-                return w1st_codes[:, P * g : P * (g + 1)], w1st_scales[:, P * g : P * (g + 1)]
-            return w23_codes[g][:, P * (t - 2) : P * (t - 1)], w23_scales[g][:, P * (t - 2) : P * (t - 1)]
-
-        def product(t, j0, j1, width, bank):
-            acc = psum.tile([P, j1 - j0], F32, name="acc%d_%d" % (t, j0), tag="bank%d" % bank)
+        def product(t, b):
+            d, u = divmod(t, 2)
+            acc = psum.tile([P, BANK], F32, name="acc%d_%d" % (t, b))
             order = range(PASSES) if t < 2 else range(PASSES - 1, -1, -1)
-            for c0 in range(0, j1 - j0, width):
-                h = 0 if j0 + c0 < EARLY else 1
-                x0 = j0 + c0 - X_PIECES[h][0]
-                for g in order:
-                    codes, scales = weights_of(t, g)
-                    nc.tensor.matmul_mx(
-                        out=acc[:, c0 : c0 + width],
-                        lhsT=codes.bitcast(FP8X4),
-                        lhsT_scale=scales,
-                        rhs=x_codes[h][:, g, 2 * x0 : 2 * (x0 + width)].bitcast(FP4X4),
-                        rhs_scale=x_sc[h][:, g, x0 : x0 + width],
-                        start=(g == order[0]),
-                        stop=(g == order[-1]),
-                    )
+            for g in order:
+                nc.tensor.matmul_mx(
+                    out=acc[:],
+                    lhsT=w_codes[d][g][:, P * u : P * (u + 1)].bitcast(FP8X4),
+                    lhsT_scale=w_scales[d][g][:, P * u : P * (u + 1)],
+                    rhs=x_codes[g][:, 2 * BANK * b : 2 * BANK * (b + 1)].bitcast(FP4X4),
+                    rhs_scale=x_sc[:, g, BANK * b : BANK * (b + 1)],
+                    start=(g == order[0]),
+                    stop=(g == order[-1]),
+                )
             return acc
 
-        for g in range(PASSES):
-            deal_pairs(nc.vector.tensor_copy, w0_bf[g][:], 0, g)
-            deal_23(nc.vector.tensor_copy, 0, g)
-            quantize(w0_codes[g], w0_scales[g], w0_bf[g], 0, P)
-            quantize_23(0, g)
-        nc.scalar.copy(out=y[0][:, 0:BANK], in_=product(0, 0, BANK, BANK, 0)[:])
-        nc.vector.tensor_copy(out=y[0][:, BANK:EARLY], in_=product(0, BANK, EARLY, P, 1)[:])
+        for t in range(PACK):
+            for b in range(T // BANK):
+                copy = nc.vector.tensor_copy if (t, b) == (0, 1) else nc.scalar.copy
+                copy(out=y[t][:, BANK * b : BANK * (b + 1)], in_=product(t, b)[:])
 
-        for g in range(PASSES):
-            deal_23(nc.scalar.copy, 1, g)
-            deal_pairs(nc.scalar.copy, w1st_bf[:, PACK * P * g : PACK * P * (g + 1)], 1, g)
-        for g in range(PASSES):
-            quantize_23(1, g)
-        quantize(w1st_codes, w1st_scales, w1st_bf, 0, PASSES * P)
-        y_late = keep.tile([P, LATE], F32, name="y_late")
-        nc.scalar.copy(out=y_late[:], in_=product(0, EARLY, T, P, 0)[:])
-        y_first = keep.tile([P, FIRST], F32, name="y_first", tag="turned1")
-        nc.scalar.copy(out=y_first[:], in_=product(2, 0, FIRST, P, 1)[:])
-        for t, j0, j1, width, bank in (
-            (1, 0, 512, BANK, 2),
-            (1, 512, 768, P, 3),
-            (1, 768, 896, P, 0),
-            (1, 896, 1024, P, 1),
-        ):
-            nc.scalar.copy(out=y[t][:, j0:j1], in_=product(t, j0, j1, width, bank)[:])
-
-        def by_col(c0, c1):
-            g0 = max(g for g in grouped if g <= c0)
-            return grouped[g0][:].rearrange("p (c d v) -> p c d v", d=2, v=2)[:, c0 - g0 : c1 - g0]
-
-        def scatter(t, values, j0, j1):
-            nc.vector.tensor_copy(window[t][:].indirect(offsets[:, j0 // LIST_ROWS : j1 // LIST_ROWS]), values)
-
-        def store(t):
+        def scatter(t):
+            if t % 2 == 0:
+                nc.vector.tensor_copy(window[t][:].indirect(offsets[:]), y[t][:])
+            else:
+                for j0, j1 in SCALAR_SCATTERS:
+                    nc.scalar.activation(window[t][:].indirect(offsets[:, j0 // LIST_ROWS : j1 // LIST_ROWS]), y[t][:, j0:j1], COPY)
             nc.sync.dma_start(out=rows_of(out_0, t), in_=window[t][:])
 
-        def turn(t, b):
-            acc = psum.tile([P, BANK], F32, name="turn%d_%d" % (t, b), tag="bank%d" % TURN_ORDER.index(b))
-            for j in range(BANK // P):
-                nc.tensor.transpose(acc[:, P * j : P * (j + 1)], window[t][:, BANK * b + P * j : BANK * b + P * (j + 1)], ident[:])
-            dst = turned[b][:].rearrange("p (j s m) -> p j s m", s=2, m=P)[:, :, t, :]
-            nc.scalar.copy(out=dst, in_=acc[:].rearrange("p (j m) -> p j m", m=P))
+        def pair_view(d, c0, c1):
+            h = 0 if c0 < SPLIT else 1
+            base = halves[h][0]
+            return pairs[h][:].rearrange("p (d c v) -> p d c v", d=2, v=2)[:, d, c0 - base : c1 - base]
 
-        def turn_back(b):
-            acc = psum.tile([P, BANK], F32, name="back%d" % b, tag="bank%d" % (4 + b))
-            words = turned[b][:].bitcast(F32)
-            for j in range(BANK // P):
-                nc.tensor.transpose(acc[:, P * j : P * (j + 1)], words[:, P * j : P * (j + 1)], ident[:])
-            c0, c1 = BANK * b, BANK * (b + 1)
-            if c0 == GROUPS[0][0]:
-                nc.scalar.copy(out=by_col(c0, c1)[:, :, 0, :], in_=acc[:].bitcast(BF16).rearrange("p (c v) -> p c v", v=2))
-            else:
-                g0 = max(g for g in grouped if g <= c0)
-                dst = grouped[g0][:].bitcast(F32).rearrange("p (c d) -> p c d", d=2)[:, c0 - g0 : c1 - g0]
-                nc.scalar.copy(out=dst, in_=acc[:].unsqueeze(2).to_broadcast([P, BANK, 2]))
+        def round_into(copy, t, c0, c1):
+            copy(out=pair_view(t // 2, c0, c1)[:, :, t % 2], in_=window[t][:, c0:c1])
 
-        scatter(0, y[0][:, 0:EARLY], 0, EARLY)
-        scatter(0, y_late[:], EARLY, T)
-        store(0)
-        scatter(2, y_first[:], 0, FIRST)
-        turned = [keep.tile([P, 2 * BANK], BF16, name="turned%d" % b, tag="turned%d" % b) for b in range(U // BANK)]
-        for b in TURN_ORDER:
-            turn(0, b)
-        for t, j0, j1, width, bank in (
-            (2, 256, 512, P, 0),
-            (2, 512, 768, P, 1),
-            (2, 768, 896, P, 2),
-            (2, 896, 1024, P, 3),
-            (3, 0, 512, BANK, 0),
-            (3, 512, 768, P, 1),
-            (3, 768, 896, P, 2),
-            (3, 896, 1024, P, 3),
-        ):
-            nc.scalar.copy(out=y[t][:, j0:j1], in_=product(t, j0, j1, width, bank)[:])
+        for t in range(2):
+            scatter(t)
+            for c0, c1 in halves:
+                round_into(gpsimd_copy, t, c0, c1)
+        scatter(2)
+        round_into(nc.vector.tensor_copy, 2, 0, SPLIT)
+        nc.vector.tensor_copy(out=pair_view(1, SPLIT, U), in_=window[2][:, SPLIT:U].unsqueeze(2).to_broadcast([P, U - SPLIT, 2]))
+        scatter(3)
 
-        scatter(1, y[1][:], 0, T)
-        store(1)
-        for b in TURN_ORDER:
-            turn(1, b)
-        for b in TURN_ORDER:
-            turn_back(b)
-
-        scatter(2, y[2][:, FIRST:T], FIRST, T)
-        store(2)
-        for copy, (c0, c1) in zip((gpsimd_copy, gpsimd_copy, nc.scalar.copy), GROUPS):
-            copy(out=by_col(c0, c1)[:, :, 1, :], in_=window[2][:, c0:c1].unsqueeze(2).to_broadcast([P, c1 - c0, 2]))
-
-        scatter(3, y[3][:], 0, T)
-        store(3)
         words_out = out_1[0].rearrange("p c r -> p (c r)").bitcast(I32)
 
-        def round_last(copy, c0, c1):
-            copy(out=by_col(c0, c1)[:, :, 1, 1], in_=window[3][:, c0:c1])
+        def group_view(c0, c1):
+            h = 0 if c0 < SPLIT else 1
+            base = halves[h][0]
+            return grouped[h][:, PACK * (c0 - base) : PACK * (c1 - base)]
+
+        def weave(copy, word, c0, c1):
+            h = 0 if c0 < SPLIT else 1
+            base = halves[h][0]
+            src = pairs[h][:].bitcast(word).rearrange("p (d c) -> p c d", d=2)[:, c0 - base : c1 - base]
+            copy(out=group_view(c0, c1).bitcast(word).rearrange("p (c d) -> p c d", d=2), in_=src)
 
         def quantize_out(s0, s1):
             for c0 in range(s0, s1, QUANT):
@@ -246,14 +153,18 @@ def tile_picked_wkvput_none_lo_kernel(tc, x_words, x_scales, mem, w1, slot, out_
                 nc.vector.quantize_mx(
                     out=out_codes[:, c0 : c0 + QUANT].bitcast(FP8X4),
                     scales=out_scales[4 * b :, d0 : d0 + QUANT],
-                    in_=by_col(c0, c0 + QUANT).rearrange("p c d v -> p (c d v)"),
+                    in_=group_view(c0, c0 + QUANT),
                 )
             nc.sync.dma_start(out=words_out[:, s0:s1], in_=out_codes[:, s0:s1].bitcast(I32))
 
-        for c0, c1 in SCALAR_PIECES:
-            round_last(nc.scalar.copy, c0, c1)
-        for c0 in range(0, 1024, QUANT):
-            round_last(nc.vector.tensor_copy, c0, c0 + QUANT)
+        round_into(nc.scalar.copy, 3, 1024, 1536)
+        round_into(nc.scalar.copy, 3, 1536, 2048)
+        for c0, c1 in STORE_PIECES[2:]:
+            weave(nc.scalar.copy, U32, c0, c1)
+        for c0, c1 in STORE_PIECES[:2]:
+            round_into(nc.vector.tensor_copy, 3, c0, c1)
+        for c0, c1 in STORE_PIECES[:2]:
+            weave(nc.vector.tensor_copy, I32, c0, c1)
         for s0, s1 in STORE_PIECES:
             quantize_out(s0, s1)
         for q in (0, 2, 1, 3):

@@ -20,7 +20,6 @@ PACK = 4
 PASSES = K // (P * PACK)
 BANK = 512
 LIST_ROWS = 16
-SCALAR_SCATTERS = ((0, 384), (384, 768), (768, 1024))
 SPLIT = 1024
 QUANT = 256
 STORE_PIECES = ((0, 512), (512, 1024), (1024, 1536), (1536, 1792), (1792, 2048))
@@ -91,7 +90,7 @@ def tile_picked_wkvput_none_lo_kernel(tc, x_words, x_scales, mem, w1, slot, out_
         def product(t, b):
             d, u = divmod(t, 2)
             acc = psum.tile([P, BANK], F32, name="acc%d_%d" % (t, b))
-            order = range(PASSES) if t < 2 else range(PASSES - 1, -1, -1)
+            order = range(PASSES) if t < 3 else range(PASSES - 1, -1, -1)
             for g in order:
                 nc.tensor.matmul_mx(
                     out=acc[:],
@@ -106,15 +105,17 @@ def tile_picked_wkvput_none_lo_kernel(tc, x_words, x_scales, mem, w1, slot, out_
 
         for t in range(PACK):
             for b in range(T // BANK):
-                copy = nc.vector.tensor_copy if (t, b) == (0, 1) else nc.scalar.copy
+                copy = nc.vector.tensor_copy if (t, b) in ((0, 0), (0, 1)) else nc.scalar.copy
                 copy(out=y[t][:, BANK * b : BANK * (b + 1)], in_=product(t, b)[:])
 
-        def scatter(t):
-            if t % 2 == 0:
-                nc.vector.tensor_copy(window[t][:].indirect(offsets[:]), y[t][:])
+        def scatter(engine, t, j0, j1):
+            target = window[t][:].indirect(offsets[:, j0 // LIST_ROWS : j1 // LIST_ROWS])
+            if engine == "vector":
+                nc.vector.tensor_copy(target, y[t][:, j0:j1])
             else:
-                for j0, j1 in SCALAR_SCATTERS:
-                    nc.scalar.activation(window[t][:].indirect(offsets[:, j0 // LIST_ROWS : j1 // LIST_ROWS]), y[t][:, j0:j1], COPY)
+                nc.scalar.activation(target, y[t][:, j0:j1], COPY)
+
+        def store(t):
             nc.sync.dma_start(out=rows_of(out_0, t), in_=window[t][:])
 
         def pair_view(d, c0, c1):
@@ -125,14 +126,26 @@ def tile_picked_wkvput_none_lo_kernel(tc, x_words, x_scales, mem, w1, slot, out_
         def round_into(copy, t, c0, c1):
             copy(out=pair_view(t // 2, c0, c1)[:, :, t % 2], in_=window[t][:, c0:c1])
 
+        def round_twice(copy, t, c0, c1):
+            copy(out=pair_view(t // 2, c0, c1), in_=window[t][:, c0:c1].unsqueeze(2).to_broadcast([P, c1 - c0, 2]))
+
+        scatter("vector", 0, 0, T)
+        store(0)
+        scatter("scalar", 1, 0, 384)
+        scatter("vector", 1, 384, T)
+        store(1)
+        scatter("scalar", 2, 0, 256)
+        scatter("scalar", 2, 256, 512)
+        scatter("vector", 2, 512, T)
+        store(2)
+        for j0, j1 in ((0, 384), (384, 768), (768, T)):
+            scatter("scalar", 3, j0, j1)
+        store(3)
         for t in range(2):
-            scatter(t)
             for c0, c1 in halves:
                 round_into(gpsimd_copy, t, c0, c1)
-        scatter(2)
+        round_twice(nc.vector.tensor_copy, 2, SPLIT, U)
         round_into(nc.vector.tensor_copy, 2, 0, SPLIT)
-        nc.vector.tensor_copy(out=pair_view(1, SPLIT, U), in_=window[2][:, SPLIT:U].unsqueeze(2).to_broadcast([P, U - SPLIT, 2]))
-        scatter(3)
 
         words_out = out_1[0].rearrange("p c r -> p (c r)").bitcast(I32)
 
@@ -169,5 +182,4 @@ def tile_picked_wkvput_none_lo_kernel(tc, x_words, x_scales, mem, w1, slot, out_
             quantize_out(s0, s1)
         for q in (0, 2, 1, 3):
             rows = out_2[0, 4 * q : 4 * q + 4, :].bitcast(I32).rearrange("r (j c) -> j r c", j=4)
-            queue = nc.sync if q < 2 else nc.scalar
-            queue.dma_start(out=rows, in_=out_scales[32 * q : 32 * q + 16, :].bitcast(I32))
+            nc.sync.dma_start(out=rows, in_=out_scales[32 * q : 32 * q + 16, :].bitcast(I32))

@@ -20,6 +20,7 @@ PACK = 4
 PASSES = K // (P * PACK)
 BANK = 512
 LIST_ROWS = 16
+W_PIECES = (((0, 512),), ((0, 256), (256, 512)))
 SPLIT = 1024
 QUANT = 256
 STORE_PIECES = ((0, 512), (512, 1024), (1024, 1536), (1536, 1792), (1792, 2048))
@@ -37,7 +38,7 @@ def tile_picked_wkvput_none_lo_kernel(tc, x_words, x_scales, mem, w1, slot, out_
             )
 
         offsets = keep.tile([P, T // LIST_ROWS], U16, name="offsets")
-        w_raw = [keep.tile([P, PACK, N], F32, name="w_raw%d" % g) for g in range(PASSES)]
+        w_raw = {(g, s): keep.tile([P, PACK, n1 - n0], F32, name="w_raw%d_%d" % (g, s)) for g in range(PASSES) for s, (n0, n1) in enumerate(W_PIECES[g])}
         w_bf = [[keep.tile([P, 2 * PACK * P], BF16, name="w_bf%d_%d" % (d, g), align_bytes=64) for g in range(PASSES)] for d in range(2)]
         w_codes = [[keep.tile([P, 2 * P], U32, name="w_codes%d_%d" % (d, g), align_bytes=64) for g in range(PASSES)] for d in range(2)]
         w_scales = [[keep.tile([P, 2 * P], U8, name="w_scales%d_%d" % (d, g), align_bytes=64) for g in range(PASSES)] for d in range(2)]
@@ -55,8 +56,9 @@ def tile_picked_wkvput_none_lo_kernel(tc, x_words, x_scales, mem, w1, slot, out_
             return dram.rearrange("(p r) c -> p r c", r=PACK)[:, t, :]
 
         def load_w(g):
-            rows = w1[P * PACK * g : P * PACK * (g + 1), :]
-            nc.sync.dma_start(out=w_raw[g][:], in_=rows.rearrange("(p j) n -> p j n", j=PACK))
+            for s, (n0, n1) in enumerate(W_PIECES[g]):
+                rows = w1[P * PACK * g : P * PACK * (g + 1), n0:n1]
+                nc.sync.dma_start(out=w_raw[g, s][:], in_=rows.rearrange("(p j) n -> p j n", j=PACK))
 
         def load_x_words(g):
             nc.sync.dma_start(out=x_codes[g][:].bitcast(I32), in_=x_words[g].bitcast(I32))
@@ -74,9 +76,10 @@ def tile_picked_wkvput_none_lo_kernel(tc, x_words, x_scales, mem, w1, slot, out_
             nc.sync.dma_start(out=window[t][:], in_=rows_of(mem, t))
 
         def deal(copy, d, g):
-            dst = w_bf[d][g][:].rearrange("p (u m j) -> p m j u", u=2, j=PACK)
-            src = w_raw[g][:].rearrange("p j (m r) -> p m j r", r=PACK)[:, :, :, 2 * d : 2 * d + 2]
-            copy(out=dst, in_=src)
+            for s, (n0, n1) in enumerate(W_PIECES[g]):
+                dst = w_bf[d][g][:].rearrange("p (u m j) -> p m j u", u=2, j=PACK)[:, n0 // PACK : n1 // PACK]
+                src = w_raw[g, s][:].rearrange("p j (m r) -> p m j r", r=PACK)[:, :, :, 2 * d : 2 * d + 2]
+                copy(out=dst, in_=src)
 
         def quantize_w(d, g):
             nc.vector.quantize_mx(out=w_codes[d][g][:].bitcast(FP8X4), scales=w_scales[d][g][:], in_=w_bf[d][g][:])
@@ -90,7 +93,7 @@ def tile_picked_wkvput_none_lo_kernel(tc, x_words, x_scales, mem, w1, slot, out_
         def product(t, b):
             d, u = divmod(t, 2)
             acc = psum.tile([P, BANK], F32, name="acc%d_%d" % (t, b))
-            order = range(PASSES) if t < 3 else range(PASSES - 1, -1, -1)
+            order = range(PASSES) if 2 * t + b < 5 else range(PASSES - 1, -1, -1)
             for g in order:
                 nc.tensor.matmul_mx(
                     out=acc[:],
@@ -105,7 +108,7 @@ def tile_picked_wkvput_none_lo_kernel(tc, x_words, x_scales, mem, w1, slot, out_
 
         for t in range(PACK):
             for b in range(T // BANK):
-                copy = nc.vector.tensor_copy if (t, b) in ((0, 0), (0, 1)) else nc.scalar.copy
+                copy = nc.vector.tensor_copy if (t, b) in ((0, 0), (1, 0)) else nc.scalar.copy
                 copy(out=y[t][:, BANK * b : BANK * (b + 1)], in_=product(t, b)[:])
 
         def scatter(engine, t, j0, j1):
@@ -144,7 +147,8 @@ def tile_picked_wkvput_none_lo_kernel(tc, x_words, x_scales, mem, w1, slot, out_
         for t in range(2):
             for c0, c1 in halves:
                 round_into(gpsimd_copy, t, c0, c1)
-        round_twice(nc.vector.tensor_copy, 2, SPLIT, U)
+        round_into(nc.vector.tensor_copy, 2, SPLIT + 16, U)
+        round_twice(nc.vector.tensor_copy, 2, SPLIT, SPLIT + 16)
         round_into(nc.vector.tensor_copy, 2, 0, SPLIT)
 
         words_out = out_1[0].rearrange("p c r -> p (c r)").bitcast(I32)

@@ -21,9 +21,11 @@ PASSES = K // (P * PACK)
 BANK = 512
 LIST_ROWS = 16
 W_PIECES = (((0, 512),), ((0, 256), (256, 512)))
+SHARED = 88
 SPLIT = 1024
 QUANT = 256
-STORE_PIECES = ((0, 512), (512, 1024), (1024, 1536), (1536, 1792), (1792, 2048))
+STORE_PIECES = ((0, 512), (512, 1024), (1024, 1536), (1536, 2048))
+WEAVE_PIECES = ((1024, 1536), (1536, 1792), (1792, 2048))
 
 
 def tile_picked_wkvput_none_lo_kernel(tc, x_words, x_scales, mem, w1, slot, out_0, out_1, out_2):
@@ -68,27 +70,36 @@ def tile_picked_wkvput_none_lo_kernel(tc, x_words, x_scales, mem, w1, slot, out_
             rows = x_scales[:, 4 * q : 4 * q + 4, :].rearrange("g r n -> r g n")
             nc.sync.dma_start(out=x_sc[32 * q : 32 * q + 4, :, :].bitcast(I32), in_=rows.bitcast(I32))
         load_x_words(0)
+        nc.sync.dma_start(offsets[:], slot)
         load_w(1)
         load_x_words(1)
         nc.sync.dma_start(out=window[0][:], in_=rows_of(mem, 0))
-        nc.sync.dma_start(offsets[:], slot)
         for t in range(1, PACK):
             nc.sync.dma_start(out=window[t][:], in_=rows_of(mem, t))
 
-        def deal(copy, d, g):
-            for s, (n0, n1) in enumerate(W_PIECES[g]):
-                dst = w_bf[d][g][:].rearrange("p (u m j) -> p m j u", u=2, j=PACK)[:, n0 // PACK : n1 // PACK]
-                src = w_raw[g, s][:].rearrange("p j (m r) -> p m j r", r=PACK)[:, :, :, 2 * d : 2 * d + 2]
-                copy(out=dst, in_=src)
+        def deal(copy, d, g, s, m0, m1):
+            n0 = W_PIECES[g][s][0]
+            dst = w_bf[d][g][:].rearrange("p (u m j) -> p m j u", u=2, j=PACK)[:, n0 // PACK + m0 : n0 // PACK + m1]
+            src = w_raw[g, s][:].rearrange("p j (m r) -> p m j r", r=PACK)[:, m0:m1, :, 2 * d : 2 * d + 2]
+            copy(out=dst, in_=src)
 
-        def quantize_w(d, g):
-            nc.vector.quantize_mx(out=w_codes[d][g][:].bitcast(FP8X4), scales=w_scales[d][g][:], in_=w_bf[d][g][:])
+        def quantize_w(d, g, c0, c1):
+            nc.vector.quantize_mx(
+                out=w_codes[d][g][:, c0:c1].bitcast(FP8X4), scales=w_scales[d][g][:, c0:c1], in_=w_bf[d][g][:, PACK * c0 : PACK * c1]
+            )
 
-        for g in range(PASSES):
-            deal(nc.vector.tensor_copy, 0, g)
-            deal(nc.scalar.copy, 1, g)
-            quantize_w(0, g)
-            quantize_w(1, g)
+        deal(nc.vector.tensor_copy, 0, 0, 0, 0, SHARED)
+        deal(nc.scalar.copy, 0, 0, 0, SHARED, P)
+        deal(nc.scalar.copy, 1, 0, 0, 0, P)
+        for u in range(2):
+            quantize_w(0, 0, P * u, P * (u + 1))
+        quantize_w(1, 0, 0, 2 * P)
+        for s, (n0, n1) in enumerate(W_PIECES[1]):
+            deal(nc.vector.tensor_copy, 0, 1, s, 0, P // 2)
+            deal(nc.scalar.copy, 1, 1, s, 0, P // 2)
+            for u in range(2):
+                quantize_w(0, 1, P * u + n0 // PACK, P * u + n1 // PACK)
+        quantize_w(1, 1, 0, 2 * P)
 
         def product(t, b):
             d, u = divmod(t, 2)
@@ -138,8 +149,8 @@ def tile_picked_wkvput_none_lo_kernel(tc, x_words, x_scales, mem, w1, slot, out_
         scatter("vector", 1, 384, T)
         store(1)
         scatter("scalar", 2, 0, 256)
-        scatter("scalar", 2, 256, 512)
-        scatter("vector", 2, 512, T)
+        scatter("scalar", 2, 256, 544)
+        scatter("vector", 2, 544, T)
         store(2)
         for j0, j1 in ((0, 384), (384, 768), (768, T)):
             scatter("scalar", 3, j0, j1)
@@ -176,7 +187,7 @@ def tile_picked_wkvput_none_lo_kernel(tc, x_words, x_scales, mem, w1, slot, out_
 
         round_into(nc.scalar.copy, 3, 1024, 1536)
         round_into(nc.scalar.copy, 3, 1536, 2048)
-        for c0, c1 in STORE_PIECES[2:]:
+        for c0, c1 in WEAVE_PIECES:
             weave(nc.scalar.copy, U32, c0, c1)
         for c0, c1 in STORE_PIECES[:2]:
             round_into(nc.vector.tensor_copy, 3, c0, c1)
@@ -186,4 +197,5 @@ def tile_picked_wkvput_none_lo_kernel(tc, x_words, x_scales, mem, w1, slot, out_
             quantize_out(s0, s1)
         for q in (0, 2, 1, 3):
             rows = out_2[0, 4 * q : 4 * q + 4, :].bitcast(I32).rearrange("r (j c) -> j r c", j=4)
-            nc.sync.dma_start(out=rows, in_=out_scales[32 * q : 32 * q + 16, :].bitcast(I32))
+            queue = nc.sync if q < 2 else nc.scalar
+            queue.dma_start(out=rows, in_=out_scales[32 * q : 32 * q + 16, :].bitcast(I32))

@@ -20,7 +20,6 @@ PACK = 4
 PASSES = K // (P * PACK)
 BANK = 512
 LIST_ROWS = 16
-W_PIECES = (((0, 512),), ((0, 256), (256, 512)))
 SHARED = 88
 SPLIT = 1024
 QUANT = 256
@@ -40,7 +39,8 @@ def tile_picked_wkvput_none_lo_kernel(tc, x_words, x_scales, mem, w1, slot, out_
             )
 
         offsets = keep.tile([P, T // LIST_ROWS], U16, name="offsets")
-        w_raw = {(g, s): keep.tile([P, PACK, n1 - n0], F32, name="w_raw%d_%d" % (g, s)) for g in range(PASSES) for s, (n0, n1) in enumerate(W_PIECES[g])}
+        w_first = keep.tile([P, PACK, N], F32, name="w_first")
+        w_second = [keep.tile([P, 2, N], F32, name="w_second%d" % e) for e in range(2)]
         w_bf = [[keep.tile([P, 2 * PACK * P], BF16, name="w_bf%d_%d" % (d, g), align_bytes=64) for g in range(PASSES)] for d in range(2)]
         w_codes = [[keep.tile([P, 2 * P], U32, name="w_codes%d_%d" % (d, g), align_bytes=64) for g in range(PASSES)] for d in range(2)]
         w_scales = [[keep.tile([P, 2 * P], U8, name="w_scales%d_%d" % (d, g), align_bytes=64) for g in range(PASSES)] for d in range(2)]
@@ -57,30 +57,27 @@ def tile_picked_wkvput_none_lo_kernel(tc, x_words, x_scales, mem, w1, slot, out_
         def rows_of(dram, t):
             return dram.rearrange("(p r) c -> p r c", r=PACK)[:, t, :]
 
-        def load_w(g):
-            for s, (n0, n1) in enumerate(W_PIECES[g]):
-                rows = w1[P * PACK * g : P * PACK * (g + 1), n0:n1]
-                nc.sync.dma_start(out=w_raw[g, s][:], in_=rows.rearrange("(p j) n -> p j n", j=PACK))
+        w_rows = w1.rearrange("(g p j) n -> g p j n", g=PASSES, j=PACK)
 
         def load_x_words(g):
             nc.sync.dma_start(out=x_codes[g][:].bitcast(I32), in_=x_words[g].bitcast(I32))
 
-        load_w(0)
+        nc.sync.dma_start(out=w_first[:], in_=w_rows[0])
         for q in (0, 2, 1, 3):
             rows = x_scales[:, 4 * q : 4 * q + 4, :].rearrange("g r n -> r g n")
             nc.sync.dma_start(out=x_sc[32 * q : 32 * q + 4, :, :].bitcast(I32), in_=rows.bitcast(I32))
         load_x_words(0)
         nc.sync.dma_start(offsets[:], slot)
-        load_w(1)
+        for e in range(2):
+            nc.sync.dma_start(out=w_second[e][:], in_=w_rows[1][:, 2 * e : 2 * e + 2, :])
         load_x_words(1)
         nc.sync.dma_start(out=window[0][:], in_=rows_of(mem, 0))
         for t in range(1, PACK):
             nc.sync.dma_start(out=window[t][:], in_=rows_of(mem, t))
 
-        def deal(copy, d, g, s, m0, m1):
-            n0 = W_PIECES[g][s][0]
-            dst = w_bf[d][g][:].rearrange("p (u m j) -> p m j u", u=2, j=PACK)[:, n0 // PACK + m0 : n0 // PACK + m1]
-            src = w_raw[g, s][:].rearrange("p j (m r) -> p m j r", r=PACK)[:, m0:m1, :, 2 * d : 2 * d + 2]
+        def deal(copy, d, g, raw, j0, m0, m1):
+            dst = w_bf[d][g][:].rearrange("p (u m j) -> p m j u", u=2, j=PACK)[:, m0:m1, j0 : j0 + raw.shape[1]]
+            src = raw[:].rearrange("p j (m r) -> p m j r", r=PACK)[:, m0:m1, :, 2 * d : 2 * d + 2]
             copy(out=dst, in_=src)
 
         def quantize_w(d, g, c0, c1):
@@ -88,18 +85,16 @@ def tile_picked_wkvput_none_lo_kernel(tc, x_words, x_scales, mem, w1, slot, out_
                 out=w_codes[d][g][:, c0:c1].bitcast(FP8X4), scales=w_scales[d][g][:, c0:c1], in_=w_bf[d][g][:, PACK * c0 : PACK * c1]
             )
 
-        deal(nc.vector.tensor_copy, 0, 0, 0, 0, SHARED)
-        deal(nc.scalar.copy, 0, 0, 0, SHARED, P)
-        deal(nc.scalar.copy, 1, 0, 0, 0, P)
-        for u in range(2):
-            quantize_w(0, 0, P * u, P * (u + 1))
-        quantize_w(1, 0, 0, 2 * P)
-        for s, (n0, n1) in enumerate(W_PIECES[1]):
-            deal(nc.vector.tensor_copy, 0, 1, s, 0, P // 2)
-            deal(nc.scalar.copy, 1, 1, s, 0, P // 2)
+        deal(nc.vector.tensor_copy, 0, 0, w_first, 0, 0, SHARED)
+        deal(nc.scalar.copy, 0, 0, w_first, 0, SHARED, P)
+        deal(nc.scalar.copy, 1, 0, w_first, 0, 0, P)
+        for e in range(2):
+            deal(nc.vector.tensor_copy, 0, 1, w_second[e], 2 * e, 0, P)
+            deal(nc.scalar.copy, 1, 1, w_second[e], 2 * e, 0, P)
+        for g in range(PASSES):
             for u in range(2):
-                quantize_w(0, 1, P * u + n0 // PACK, P * u + n1 // PACK)
-        quantize_w(1, 1, 0, 2 * P)
+                quantize_w(0, g, P * u, P * (u + 1))
+            quantize_w(1, g, 0, 2 * P)
 
         def product(t, b):
             d, u = divmod(t, 2)

@@ -44,7 +44,8 @@ def tile_picked_wkvput_none_lo_kernel(tc, x_words, x_scales, mem, w1, slot, out_
         w_bf = [[keep.tile([P, 2 * PACK * P], BF16, name="w_bf%d_%d" % (d, g), align_bytes=64) for g in range(PASSES)] for d in range(2)]
         w_codes = [[keep.tile([P, 2 * P], U32, name="w_codes%d_%d" % (d, g), align_bytes=64) for g in range(PASSES)] for d in range(2)]
         w_scales = [[keep.tile([P, 2 * P], U8, name="w_scales%d_%d" % (d, g), align_bytes=64) for g in range(PASSES)] for d in range(2)]
-        x_codes = [keep.tile([P, 2 * T], U8, name="x_codes%d" % g, align_bytes=64) for g in range(PASSES)]
+        x_first = [keep.tile([P, 2 * BANK], U8, name="x_first%d" % b, align_bytes=64) for b in range(T // BANK)]
+        x_second = keep.tile([P, 2 * T], U8, name="x_second", align_bytes=64)
         x_sc = keep.tile([P, PASSES, T], U8, name="x_sc", align_bytes=64)
         window = [keep.tile([P, U], F32, name="window%d" % t) for t in range(PACK)]
         y = [keep.tile([P, T], F32, name="y%d" % t) for t in range(PACK)]
@@ -59,18 +60,19 @@ def tile_picked_wkvput_none_lo_kernel(tc, x_words, x_scales, mem, w1, slot, out_
 
         w_rows = w1.rearrange("(g p j) n -> g p j n", g=PASSES, j=PACK)
 
-        def load_x_words(g):
-            nc.sync.dma_start(out=x_codes[g][:].bitcast(I32), in_=x_words[g].bitcast(I32))
+        def load_x_first(b):
+            nc.sync.dma_start(out=x_first[b][:].bitcast(I32), in_=x_words[0][:, 2 * BANK * b : 2 * BANK * (b + 1)].bitcast(I32))
 
         nc.sync.dma_start(out=w_first[:], in_=w_rows[0])
         for q in (0, 2, 1, 3):
             rows = x_scales[:, 4 * q : 4 * q + 4, :].rearrange("g r n -> r g n")
             nc.sync.dma_start(out=x_sc[32 * q : 32 * q + 4, :, :].bitcast(I32), in_=rows.bitcast(I32))
-        load_x_words(0)
-        nc.sync.dma_start(offsets[:], slot)
+        load_x_first(0)
         for e in range(2):
             nc.sync.dma_start(out=w_second[e][:], in_=w_rows[1][:, 2 * e : 2 * e + 2, :])
-        load_x_words(1)
+        load_x_first(1)
+        nc.sync.dma_start(offsets[:], slot)
+        nc.sync.dma_start(out=x_second[:].bitcast(I32), in_=x_words[1].bitcast(I32))
         nc.sync.dma_start(out=window[0][:], in_=rows_of(mem, 0))
         for t in range(1, PACK):
             nc.sync.dma_start(out=window[t][:], in_=rows_of(mem, t))
@@ -99,23 +101,22 @@ def tile_picked_wkvput_none_lo_kernel(tc, x_words, x_scales, mem, w1, slot, out_
         def product(t, b):
             d, u = divmod(t, 2)
             acc = psum.tile([P, BANK], F32, name="acc%d_%d" % (t, b))
-            order = range(PASSES) if 2 * t + b < 5 else range(PASSES - 1, -1, -1)
+            order = range(PASSES) if b == 0 or t == 0 else range(PASSES - 1, -1, -1)
             for g in order:
                 nc.tensor.matmul_mx(
                     out=acc[:],
                     lhsT=w_codes[d][g][:, P * u : P * (u + 1)].bitcast(FP8X4),
                     lhsT_scale=w_scales[d][g][:, P * u : P * (u + 1)],
-                    rhs=x_codes[g][:, 2 * BANK * b : 2 * BANK * (b + 1)].bitcast(FP4X4),
+                    rhs=(x_first[b][:] if g == 0 else x_second[:, 2 * BANK * b : 2 * BANK * (b + 1)]).bitcast(FP4X4),
                     rhs_scale=x_sc[:, g, BANK * b : BANK * (b + 1)],
                     start=(g == order[0]),
                     stop=(g == order[-1]),
                 )
             return acc
 
-        for t in range(PACK):
-            for b in range(T // BANK):
-                copy = nc.vector.tensor_copy if (t, b) in ((0, 0), (1, 0)) else nc.scalar.copy
-                copy(out=y[t][:, BANK * b : BANK * (b + 1)], in_=product(t, b)[:])
+        for t, b in [(0, 0), (0, 1)] + [(t, b) for b in range(T // BANK) for t in range(1, PACK)]:
+            copy = nc.vector.tensor_copy if (t, b) in ((0, 0), (1, 0)) else nc.scalar.copy
+            copy(out=y[t][:, BANK * b : BANK * (b + 1)], in_=product(t, b)[:])
 
         def scatter(engine, t, j0, j1):
             target = window[t][:].indirect(offsets[:, j0 // LIST_ROWS : j1 // LIST_ROWS])

@@ -141,12 +141,12 @@ def tile_picked_wkvput_none_lo_kernel(tc, x_words, x_scales, mem, w1, slot, out_
 
         scatter("vector", 0, 0, T)
         store(0)
-        scatter("scalar", 1, 0, 384)
-        scatter("vector", 1, 384, T)
+        scatter("scalar", 1, 0, 288)
+        scatter("scalar", 1, 288, 544)
+        scatter("vector", 1, 544, T)
         store(1)
-        scatter("scalar", 2, 0, 256)
-        scatter("scalar", 2, 256, 544)
-        scatter("vector", 2, 544, T)
+        scatter("scalar", 2, 0, 384)
+        scatter("vector", 2, 384, T)
         store(2)
         for j0, j1 in ((0, 384), (384, 768), (768, T)):
             scatter("scalar", 3, j0, j1)

@@ -50,7 +50,8 @@ def tile_picked_wkvput_none_lo_kernel(tc, x_words, x_scales, mem, w1, slot, out_
         window = [keep.tile([P, U], F32, name="window%d" % t) for t in range(PACK)]
         y = [keep.tile([P, T], F32, name="y%d" % t) for t in range(PACK)]
         halves = ((0, SPLIT), (SPLIT, U))
-        pairs = [keep.tile([P, PACK * (c1 - c0)], BF16, name="pairs%d" % c0) for c0, c1 in halves]
+        all_pairs = keep.tile([P, PACK * U], BF16, name="all_pairs")
+        pairs = [all_pairs[:, PACK * c0 : PACK * c1] for c0, c1 in halves]
         grouped = [keep.tile([P, PACK * (c1 - c0)], BF16, name="grouped%d" % c0, align_bytes=64) for c0, c1 in halves]
         out_codes = keep.tile([P, U], U32, name="out_codes", align_bytes=64)
         out_scales = keep.tile([P, BANK], U8, name="out_scales", align_bytes=64)
@@ -131,7 +132,7 @@ def tile_picked_wkvput_none_lo_kernel(tc, x_words, x_scales, mem, w1, slot, out_
         def pair_view(d, c0, c1):
             h = 0 if c0 < SPLIT else 1
             base = halves[h][0]
-            return pairs[h][:].rearrange("p (d c v) -> p d c v", d=2, v=2)[:, d, c0 - base : c1 - base]
+            return pairs[h].rearrange("p (d c v) -> p d c v", d=2, v=2)[:, d, c0 - base : c1 - base]
 
         def round_into(copy, t, c0, c1):
             copy(out=pair_view(t // 2, c0, c1)[:, :, t % 2], in_=window[t][:, c0:c1])
@@ -141,9 +142,9 @@ def tile_picked_wkvput_none_lo_kernel(tc, x_words, x_scales, mem, w1, slot, out_
 
         scatter("vector", 0, 0, T)
         store(0)
-        scatter("scalar", 1, 0, 288)
-        scatter("scalar", 1, 288, 544)
-        scatter("vector", 1, 544, T)
+        scatter("scalar", 1, 0, 256)
+        scatter("scalar", 1, 256, 512)
+        scatter("vector", 1, 512, T)
         store(1)
         scatter("scalar", 2, 0, 384)
         scatter("vector", 2, 384, T)
@@ -152,8 +153,10 @@ def tile_picked_wkvput_none_lo_kernel(tc, x_words, x_scales, mem, w1, slot, out_
             scatter("scalar", 3, j0, j1)
         store(3)
         for t in range(2):
-            for c0, c1 in halves:
-                round_into(gpsimd_copy, t, c0, c1)
+            gpsimd_copy(
+                out=all_pairs[:].rearrange("p (h d c v) -> p h d c v", h=2, d=2, v=2)[:, :, 0, :, t],
+                in_=window[t][:].rearrange("p (h c) -> p h c", h=2),
+            )
         round_into(nc.vector.tensor_copy, 2, SPLIT + 16, U)
         round_twice(nc.vector.tensor_copy, 2, SPLIT, SPLIT + 16)
         round_into(nc.vector.tensor_copy, 2, 0, SPLIT)
@@ -168,7 +171,7 @@ def tile_picked_wkvput_none_lo_kernel(tc, x_words, x_scales, mem, w1, slot, out_
         def weave(copy, word, c0, c1):
             h = 0 if c0 < SPLIT else 1
             base = halves[h][0]
-            src = pairs[h][:].bitcast(word).rearrange("p (d c) -> p c d", d=2)[:, c0 - base : c1 - base]
+            src = pairs[h].bitcast(word).rearrange("p (d c) -> p c d", d=2)[:, c0 - base : c1 - base]
             copy(out=group_view(c0, c1).bitcast(word).rearrange("p (c d) -> p c d", d=2), in_=src)
 
         def quantize_out(s0, s1):

@@ -48,10 +48,22 @@ def tile_picked_wkvput_none_lo_kernel(tc, x_words, x_scales, mem, w1, slot, out_
         x_second = keep.tile([P, 2 * T], U8, name="x_second", align_bytes=64)
         x_sc = keep.tile([P, PASSES, T], U8, name="x_sc", align_bytes=64)
         window = [keep.tile([P, U], F32, name="window%d" % t) for t in range(PACK)]
-        y = [keep.tile([P, T], F32, name="y%d" % t) for t in range(PACK)]
+        y = [keep.tile([P, T], F32, name="y%d" % t) for t in range(PACK - 1)]
         halves = ((0, SPLIT), (SPLIT, U))
-        all_pairs = keep.tile([P, PACK * U], BF16, name="all_pairs")
+        all_pairs = keep.tile([P, PACK * U + 2 * 128], BF16, name="all_pairs")
         pairs = [all_pairs[:, PACK * c0 : PACK * c1] for c0, c1 in halves]
+        y_last = {
+            0: keep.tile([P, 384], F32, name="y_last0")[:],
+            384: all_pairs[:].bitcast(F32)[:, 2 * U - 256 :],
+            768: keep.tile([P, 256], F32, name="y_last2")[:],
+        }
+
+        def y_of(t, j0, j1):
+            if t < PACK - 1:
+                return y[t][:, j0:j1]
+            base = j0 - j0 % 384
+            return y_last[base][:, j0 - base : j1 - base]
+
         grouped = [keep.tile([P, PACK * (c1 - c0)], BF16, name="grouped%d" % c0, align_bytes=64) for c0, c1 in halves]
         out_codes = keep.tile([P, U], U32, name="out_codes", align_bytes=64)
         out_scales = keep.tile([P, BANK], U8, name="out_scales", align_bytes=64)
@@ -117,14 +129,17 @@ def tile_picked_wkvput_none_lo_kernel(tc, x_words, x_scales, mem, w1, slot, out_
 
         for t, b in [(0, 0), (0, 1)] + [(t, b) for b in range(T // BANK) for t in range(1, PACK)]:
             copy = nc.vector.tensor_copy if (t, b) in ((0, 0), (1, 0)) else nc.scalar.copy
-            copy(out=y[t][:, BANK * b : BANK * (b + 1)], in_=product(t, b)[:])
+            acc = product(t, b)
+            cuts = [BANK * b, BANK * (b + 1)] if t < PACK - 1 else [BANK * b, 384 * (b + 1), BANK * (b + 1)]
+            for j0, j1 in zip(cuts, cuts[1:]):
+                copy(out=y_of(t, j0, j1), in_=acc[:, j0 - BANK * b : j1 - BANK * b])
 
         def scatter(engine, t, j0, j1):
             target = window[t][:].indirect(offsets[:, j0 // LIST_ROWS : j1 // LIST_ROWS])
             if engine == "vector":
-                nc.vector.tensor_copy(target, y[t][:, j0:j1])
+                nc.vector.tensor_copy(target, y_of(t, j0, j1))
             else:
-                nc.scalar.activation(target, y[t][:, j0:j1], COPY)
+                nc.scalar.activation(target, y_of(t, j0, j1), COPY)
 
         def store(t):
             nc.sync.dma_start(out=rows_of(out_0, t), in_=window[t][:])
@@ -154,10 +169,11 @@ def tile_picked_wkvput_none_lo_kernel(tc, x_words, x_scales, mem, w1, slot, out_
         store(3)
         for t in range(2):
             gpsimd_copy(
-                out=all_pairs[:].rearrange("p (h d c v) -> p h d c v", h=2, d=2, v=2)[:, :, 0, :, t],
+                out=all_pairs[:, : PACK * U].rearrange("p (h d c v) -> p h d c v", h=2, d=2, v=2)[:, :, 0, :, t],
                 in_=window[t][:].rearrange("p (h c) -> p h c", h=2),
             )
-        round_into(nc.vector.tensor_copy, 2, SPLIT + 16, U)
+        round_into(nc.scalar.copy, 2, U - 256, U)
+        round_into(nc.vector.tensor_copy, 2, SPLIT + 16, U - 256)
         round_twice(nc.vector.tensor_copy, 2, SPLIT, SPLIT + 16)
         round_into(nc.vector.tensor_copy, 2, 0, SPLIT)
 

@@ -50,11 +50,11 @@ def tile_picked_wkvput_none_lo_kernel(tc, x_words, x_scales, mem, w1, slot, out_
         window = [keep.tile([P, U], F32, name="window%d" % t) for t in range(PACK)]
         y = [keep.tile([P, T], F32, name="y%d" % t) for t in range(PACK - 1)]
         halves = ((0, SPLIT), (SPLIT, U))
-        all_pairs = keep.tile([P, PACK * U + 2 * 128], BF16, name="all_pairs")
+        all_pairs = keep.tile([P, PACK * U + 2 * (384 - 160)], BF16, name="all_pairs")
         pairs = [all_pairs[:, PACK * c0 : PACK * c1] for c0, c1 in halves]
         y_last = {
             0: keep.tile([P, 384], F32, name="y_last0")[:],
-            384: all_pairs[:].bitcast(F32)[:, 2 * U - 256 :],
+            384: all_pairs[:].bitcast(F32)[:, 2 * U - 160 :],
             768: keep.tile([P, 256], F32, name="y_last2")[:],
         }
 
@@ -172,8 +172,8 @@ def tile_picked_wkvput_none_lo_kernel(tc, x_words, x_scales, mem, w1, slot, out_
                 out=all_pairs[:, : PACK * U].rearrange("p (h d c v) -> p h d c v", h=2, d=2, v=2)[:, :, 0, :, t],
                 in_=window[t][:].rearrange("p (h c) -> p h c", h=2),
             )
-        round_into(nc.scalar.copy, 2, U - 256, U)
-        round_into(nc.vector.tensor_copy, 2, SPLIT + 16, U - 256)
+        round_into(nc.scalar.copy, 2, U - 160, U)
+        round_into(nc.vector.tensor_copy, 2, SPLIT + 16, U - 160)
         round_twice(nc.vector.tensor_copy, 2, SPLIT, SPLIT + 16)
         round_into(nc.vector.tensor_copy, 2, 0, SPLIT)
 

from contextlib import ExitStack

import concourse.mybir as mybir

K, T, N, U = 1024, 1024, 512, 2048
FLOPS = 2 * K * T * N

F32 = mybir.dt.float32
BF16 = mybir.dt.bfloat16
I32 = mybir.dt.int32
U32 = mybir.dt.uint32
U16 = mybir.dt.uint16
U8 = mybir.dt.uint8
FP8X4 = mybir.dt.float8_e4m3fn_x4
FP4X4 = mybir.dt.float4_e2m1fn_x4
COPY = mybir.ActivationFunctionType.Copy

P = 128
PACK = 4
PASSES = K // (P * PACK)
BANK = 512
LIST_ROWS = 16
SHARED = 88
SPLIT = 1024
QUANT = 256
STORE_PIECES = ((0, 512), (512, 1024), (1024, 1536), (1536, 2048))
WEAVE_PIECES = ((1024, 1536), (1536, 1792), (1792, 2048))


def tile_picked_wkvput_none_lo_kernel(tc, x_words, x_scales, mem, w1, slot, out_0, out_1, out_2):
    nc = tc.nc
    with ExitStack() as ctx:
        keep = ctx.enter_context(tc.tile_pool(name="keep", bufs=1))
        psum = ctx.enter_context(tc.psum_pool(name="psum", bufs=1))

        def gpsimd_copy(out, in_):
            nc.gpsimd.tensor_scalar(
                out=out, in0=in_, scalar1=1.0, scalar2=-0.0, op0=mybir.AluOpType.mult, op1=mybir.AluOpType.add
            )

        offsets = keep.tile([P, T // LIST_ROWS], U16, name="offsets")
        w_first = keep.tile([P, PACK, N], F32, name="w_first")
        w_second = [keep.tile([P, 2, N], F32, name="w_second%d" % e) for e in range(2)]
        w_bf = [[keep.tile([P, 2 * PACK * P], BF16, name="w_bf%d_%d" % (d, g), align_bytes=64) for g in range(PASSES)] for d in range(2)]
        w_codes = [[keep.tile([P, 2 * P], U32, name="w_codes%d_%d" % (d, g), align_bytes=64) for g in range(PASSES)] for d in range(2)]
        w_scales = [[keep.tile([P, 2 * P], U8, name="w_scales%d_%d" % (d, g), align_bytes=64) for g in range(PASSES)] for d in range(2)]
        x_first = [keep.tile([P, 2 * BANK], U8, name="x_first%d" % b, align_bytes=64) for b in range(T // BANK)]
        x_second = keep.tile([P, 2 * T], U8, name="x_second", align_bytes=64)
        x_sc = keep.tile([P, PASSES, T], U8, name="x_sc", align_bytes=64)
        window = [keep.tile([P, U], F32, name="window%d" % t) for t in range(PACK)]
        y = [keep.tile([P, T], F32, name="y%d" % t) for t in range(PACK - 1)]
        halves = ((0, SPLIT), (SPLIT, U))
        all_pairs = keep.tile([P, PACK * U + 2 * (384 - 160)], BF16, name="all_pairs")
        pairs = [all_pairs[:, PACK * c0 : PACK * c1] for c0, c1 in halves]
        y_last = {
            0: keep.tile([P, 384], F32, name="y_last0")[:],
            384: all_pairs[:].bitcast(F32)[:, 2 * U - 160 :],
            768: keep.tile([P, 256], F32, name="y_last2")[:],
        }

        def y_of(t, j0, j1):
            if t < PACK - 1:
                return y[t][:, j0:j1]
            base = j0 - j0 % 384
            return y_last[base][:, j0 - base : j1 - base]

        grouped = [keep.tile([P, PACK * (c1 - c0)], BF16, name="grouped%d" % c0, align_bytes=64) for c0, c1 in halves]
        out_codes = keep.tile([P, U], U32, name="out_codes", align_bytes=64)
        out_scales = keep.tile([P, BANK], U8, name="out_scales", align_bytes=64)

        def rows_of(dram, t):
            return dram.rearrange("(p r) c -> p r c", r=PACK)[:, t, :]

        w_rows = w1.rearrange("(g p j) n -> g p j n", g=PASSES, j=PACK)

        def load_x_first(b):
            nc.sync.dma_start(out=x_first[b][:].bitcast(I32), in_=x_words[0][:, 2 * BANK * b : 2 * BANK * (b + 1)].bitcast(I32))

        nc.sync.dma_start(out=w_first[:], in_=w_rows[0])
        for q in (0, 2, 1, 3):
            rows = x_scales[:, 4 * q : 4 * q + 4, :].rearrange("g r n -> r g n")
            nc.sync.dma_start(out=x_sc[32 * q : 32 * q + 4, :, :].bitcast(I32), in_=rows.bitcast(I32))
        load_x_first(0)
        for e in range(2):
            nc.sync.dma_start(out=w_second[e][:], in_=w_rows[1][:, 2 * e : 2 * e + 2, :])
        load_x_first(1)
        nc.sync.dma_start(offsets[:], slot)
        nc.sync.dma_start(out=x_second[:].bitcast(I32), in_=x_words[1].bitcast(I32))
        nc.sync.dma_start(out=window[0][:], in_=rows_of(mem, 0))
        for t in range(1, PACK):
            nc.sync.dma_start(out=window[t][:], in_=rows_of(mem, t))

        def deal(copy, d, g, raw, j0, m0, m1):
            dst = w_bf[d][g][:].rearrange("p (u m j) -> p m j u", u=2, j=PACK)[:, m0:m1, j0 : j0 + raw.shape[1]]
            src = raw[:].rearrange("p j (m r) -> p m j r", r=PACK)[:, m0:m1, :, 2 * d : 2 * d + 2]
            copy(out=dst, in_=src)

        def quantize_w(d, g, c0, c1):
            nc.vector.quantize_mx(
                out=w_codes[d][g][:, c0:c1].bitcast(FP8X4), scales=w_scales[d][g][:, c0:c1], in_=w_bf[d][g][:, PACK * c0 : PACK * c1]
            )

        deal(nc.vector.tensor_copy, 0, 0, w_first, 0, 0, SHARED)
        deal(nc.scalar.copy, 0, 0, w_first, 0, SHARED, P)
        deal(nc.scalar.copy, 1, 0, w_first, 0, 0, P)
        for e in range(2):
            deal(nc.vector.tensor_copy, 0, 1, w_second[e], 2 * e, 0, P)
            deal(nc.scalar.copy, 1, 1, w_second[e], 2 * e, 0, P)
        for g in range(PASSES):
            for u in range(2):
                quantize_w(0, g, P * u, P * (u + 1))
            quantize_w(1, g, 0, 2 * P)

        def product(t, b):
            d, u = divmod(t, 2)
            acc = psum.tile([P, BANK], F32, name="acc%d_%d" % (t, b))
            order = range(PASSES) if b == 0 or t == 0 else range(PASSES - 1, -1, -1)
            for g in order:
                nc.tensor.matmul_mx(
                    out=acc[:],
                    lhsT=w_codes[d][g][:, P * u : P * (u + 1)].bitcast(FP8X4),
                    lhsT_scale=w_scales[d][g][:, P * u : P * (u + 1)],
                    rhs=(x_first[b][:] if g == 0 else x_second[:, 2 * BANK * b : 2 * BANK * (b + 1)]).bitcast(FP4X4),
                    rhs_scale=x_sc[:, g, BANK * b : BANK * (b + 1)],
                    start=(g == order[0]),
                    stop=(g == order[-1]),
                )
            return acc

        for t, b in [(0, 0), (0, 1)] + [(t, b) for b in range(T // BANK) for t in range(1, PACK)]:
            copy = nc.vector.tensor_copy if (t, b) in ((0, 0), (1, 0)) else nc.scalar.copy
            acc = product(t, b)
            cuts = [BANK * b, BANK * (b + 1)] if t < PACK - 1 else [BANK * b, 384 * (b + 1), BANK * (b + 1)]
            for j0, j1 in zip(cuts, cuts[1:]):
                copy(out=y_of(t, j0, j1), in_=acc[:, j0 - BANK * b : j1 - BANK * b])

        def scatter(engine, t, j0, j1):
            target = window[t][:].indirect(offsets[:, j0 // LIST_ROWS : j1 // LIST_ROWS])
            if engine == "vector":
                nc.vector.tensor_copy(target, y_of(t, j0, j1))
            else:
                nc.scalar.activation(target, y_of(t, j0, j1), COPY)

        def store(t):
            nc.sync.dma_start(out=rows_of(out_0, t), in_=window[t][:])

        def pair_view(d, c0, c1):
            h = 0 if c0 < SPLIT else 1
            base = halves[h][0]
            return pairs[h].rearrange("p (d c v) -> p d c v", d=2, v=2)[:, d, c0 - base : c1 - base]

        def round_into(copy, t, c0, c1):
            copy(out=pair_view(t // 2, c0, c1)[:, :, t % 2], in_=window[t][:, c0:c1])

        def round_twice(copy, t, c0, c1):
            copy(out=pair_view(t // 2, c0, c1), in_=window[t][:, c0:c1].unsqueeze(2).to_broadcast([P, c1 - c0, 2]))

        scatter("vector", 0, 0, T)
        store(0)
        scatter("scalar", 1, 0, 256)
        scatter("scalar", 1, 256, 512)
        scatter("vector", 1, 512, T)
        store(1)
        scatter("scalar", 2, 0, 384)
        scatter("vector", 2, 384, T)
        store(2)
        for j0, j1 in ((0, 384), (384, 768), (768, T)):
            scatter("scalar", 3, j0, j1)
        store(3)
        for t in range(2):
            gpsimd_copy(
                out=all_pairs[:, : PACK * U].rearrange("p (h d c v) -> p h d c v", h=2, d=2, v=2)[:, :, 0, :, t],
                in_=window[t][:].rearrange("p (h c) -> p h c", h=2),
            )
        round_into(nc.scalar.copy, 2, U - 160, U)
        round_into(nc.vector.tensor_copy, 2, SPLIT + 16, U - 160)
        round_twice(nc.vector.tensor_copy, 2, SPLIT, SPLIT + 16)
        round_into(nc.vector.tensor_copy, 2, 0, SPLIT)

        words_out = out_1[0].rearrange("p c r -> p (c r)").bitcast(I32)

        def group_view(c0, c1):
            h = 0 if c0 < SPLIT else 1
            base = halves[h][0]
            return grouped[h][:, PACK * (c0 - base) : PACK * (c1 - base)]

        def weave(copy, word, c0, c1):
            h = 0 if c0 < SPLIT else 1
            base = halves[h][0]
            src = pairs[h].bitcast(word).rearrange("p (d c) -> p c d", d=2)[:, c0 - base : c1 - base]
            copy(out=group_view(c0, c1).bitcast(word).rearrange("p (c d) -> p c d", d=2), in_=src)

        def quantize_out(s0, s1):
            for c0 in range(s0, s1, QUANT):
                b, d0 = divmod(c0, BANK)
                nc.vector.quantize_mx(
                    out=out_codes[:, c0 : c0 + QUANT].bitcast(FP8X4),
                    scales=out_scales[4 * b :, d0 : d0 + QUANT],
                    in_=group_view(c0, c0 + QUANT),
                )
            nc.sync.dma_start(out=words_out[:, s0:s1], in_=out_codes[:, s0:s1].bitcast(I32))

        round_into(nc.scalar.copy, 3, 1024, 1536)
        round_into(nc.scalar.copy, 3, 1536, 2048)
        for c0, c1 in WEAVE_PIECES:
            weave(nc.scalar.copy, U32, c0, c1)
        for c0, c1 in STORE_PIECES[:2]:
            round_into(nc.vector.tensor_copy, 3, c0, c1)
        for c0, c1 in STORE_PIECES[:2]:
            weave(nc.vector.tensor_copy, I32, c0, c1)
        for s0, s1 in STORE_PIECES:
            quantize_out(s0, s1)
        for q in (0, 2, 1, 3):
            rows = out_2[0, 4 * q : 4 * q + 4, :].bitcast(I32).rearrange("r (j c) -> j r c", j=4)
            queue = nc.sync if q < 2 else nc.scalar
            queue.dma_start(out=rows, in_=out_scales[32 * q : 32 * q + 16, :].bitcast(I32))
